import numpy as np
import ml_dtypes


def mxq(x, axis, fmt="e4m3"):
    dtype, down = {"e4m3": (ml_dtypes.float8_e4m3fn, 7), "e5m2": (ml_dtypes.float8_e5m2, 14)}[fmt]
    v = np.moveaxis(np.asarray(x, np.float32).astype(ml_dtypes.bfloat16).astype(np.float64), axis, -1)
    blocks = v.reshape(v.shape[:-1] + (-1, 32))
    amax = np.abs(blocks).max(-1, keepdims=True)
    byte = np.maximum(np.where(amax > 0, np.frexp(amax)[1] - 1 + 127, 0) - down, 1)
    scale = np.exp2(byte - 127.0)
    codes = (blocks / scale).astype(np.float32).astype(dtype).astype(np.float64)
    return np.moveaxis((codes * scale).reshape(v.shape), -1, axis)


WIDE = False


def mx_kscale(k):
    if not WIDE:
        return np.ones(k)
    levels = np.array([10, -10, 5, -5, 0])
    if k % 512:
        return np.exp2(np.random.permutation(np.resize(levels, k // 32))).repeat(32)
    a = np.empty((k // 512, 16))
    for p in range(k // 512):
        a[p, :8] = np.random.permutation(np.resize(levels, 8))
        for g in range(8):
            far = levels[np.abs(levels - a[p, g]) >= 10]
            a[p, g + 8] = far[np.random.randint(len(far))]
    return np.exp2(a.ravel()).repeat(32)


def f64(x):
    return np.asarray(x).astype(np.float64)


def striped(idx):
    return np.tile(np.asarray(idx).reshape(-1, 16).T, (8, 1)).astype(np.uint16)


def unstriped(offs):
    return offs[:16].T.reshape(-1).astype(np.int64)


E2M1 = np.array([0.0, 0.5, 1.0, 1.5, 2.0, 3.0, 4.0, 6.0, -0.0, -0.5, -1.0, -1.5, -2.0, -3.0, -4.0, -6.0])


def pack_weight(w, fmt):
    k, n = w.shape
    w = f64(np.asarray(w, np.float32).astype(ml_dtypes.bfloat16)).reshape(k // 32, 32, n)
    amax = np.abs(w).max(1)
    if fmt == "e4m3":
        byte = np.frexp(amax)[1] - 1 + 127 - 7
    else:
        mant, ex = np.frexp(amax / 6.0)
        byte = np.where(mant > 0.5, ex, ex - 1) + 127
    byte = np.clip(np.where(amax > 0, byte, 1), 1, 254)
    scaled = (w * np.exp2(127.0 - byte)[:, None, :]).reshape(k, n).astype(np.float32)
    by_word = np.ascontiguousarray(scaled.reshape(k // 512, 128, 4, n).transpose(0, 1, 3, 2))
    if fmt == "e4m3":
        words = by_word.astype(ml_dtypes.float8_e4m3fn).view(np.uint8)
    else:
        c = by_word.astype(ml_dtypes.float4_e2m1fn).view(np.uint8) & 0xF
        words = (c[..., 0::2] | (c[..., 1::2] << 4)).reshape(k // 512, 128, 2 * n)
    return np.ascontiguousarray(words), np.ascontiguousarray(byte.astype(np.uint8).reshape(k // 512, 16, n))


def unpack_weight(words, scales, fmt):
    g, _, n = scales.shape
    words = np.ascontiguousarray(words).reshape(g, 128, n, -1)
    if fmt == "e4m3":
        vals = words.view(ml_dtypes.float8_e4m3fn).astype(np.float64)
    else:
        nib = np.empty((g, 128, n, 4), np.uint8)
        nib[..., 0::2] = words & 0xF
        nib[..., 1::2] = words >> 4
        vals = E2M1[nib]
    vals = vals * np.repeat(np.exp2(scales.astype(np.float64) - 127.0), 8, axis=1)[..., None]
    return vals.transpose(0, 1, 3, 2).reshape(g * 512, n)


D, T, I, J, Q = 512, 2048, 1024, 512, 128


def setup_inputs():
    n = np.random.standard_normal
    idx = np.random.permutation(T)[:I]
    idx2 = np.random.randint(0, I, J)
    idx3 = np.random.randint(0, I, J)
    fd = mx_kscale(D)
    tokp = pack_weight(n((D, T)) / fd[:, None], "e2m1")
    return {
        "qs": (n((D, Q)) * 0.8 / np.sqrt(D) * fd[:, None]).astype(np.float32),
        "qe": (n((D, Q)) * 0.8 / np.sqrt(D) * fd[:, None]).astype(np.float32),
        "tok_words": tokp[0],
        "tok_scales": tokp[1],
        "offs": striped(idx),
        "offs2": striped(idx2),
        "offs3": striped(idx3),
    }


def reference(qs, qe, tok_words, tok_scales, offs, offs2, offs3):
    idx = unstriped(offs)
    idx2 = unstriped(offs2)
    idx3 = unstriped(offs3)
    toku = unpack_weight(tok_words, tok_scales, "e2m1")
    qsq = mxq(f64(qs), 0, "e4m3")
    tokidxg = toku[:, idx]
    a = qsq.T @ tokidxg
    qeq = mxq(f64(qe), 0, "e4m3")
    b = qeq.T @ tokidxg
    s = a[:, idx2] + b[:, idx3]
    p = np.exp(s - np.max(s, axis=1, keepdims=True))
    y = p / np.sum(p, axis=1, keepdims=True) * 512.0
    return y

@@ -1,0 +1,120 @@
+from contextlib import ExitStack
+
+import concourse.mybir as mybir
+
+D, T, I, J, Q = 512, 2048, 1024, 512, 128
+FLOPS = 2 * 2 * D * Q * I
+
+F32 = mybir.dt.float32
+BF16 = mybir.dt.bfloat16
+I32 = mybir.dt.int32
+U32 = mybir.dt.uint32
+U16 = mybir.dt.uint16
+U8 = mybir.dt.uint8
+FP8X4 = mybir.dt.float8_e4m3fn_x4
+FP4X4 = mybir.dt.float4_e2m1fn_x4
+ACT = mybir.ActivationFunctionType
+ALU = mybir.AluOpType
+AX = mybir.AxisListType
+
+P = 128
+PACK = 4
+LANES = 16
+
+
+def tile_attend_spanpointer_kernel(tc, qs, qe, tok_words, tok_scales, offs, offs2, offs3, out):
+    nc = tc.nc
+    with ExitStack() as ctx:
+        sb = ctx.enter_context(tc.tile_pool(name="sb", bufs=1))
+        ps = ctx.enter_context(tc.psum_pool(name="ps", bufs=1))
+
+        words = sb.tile([P, T], U16, name="words", align_bytes=64)
+        scales = sb.tile([P, T], U8, name="scales", align_bytes=64)
+        tok_list = sb.tile([P, I // LANES], U16, name="tok_list")
+        start_list = sb.tile([P, J // LANES], U16, name="start_list")
+        end_list = sb.tile([P, J // LANES], U16, name="end_list")
+        qs_raw = sb.tile([P, PACK, Q], F32, name="qs_raw")
+        qe_raw = sb.tile([P, PACK, Q], F32, name="qe_raw")
+
+        nc.vector.memset(scales[:].bitcast(I32), 0)
+        nc.sync.dma_start(out=words[:].bitcast(I32), in_=tok_words[0].bitcast(I32))
+        nc.sync.dma_start(tok_list[:], offs)
+        for g in range(4):
+            nc.sync.dma_start(out=scales[32 * g : 32 * g + 4, :].bitcast(I32), in_=tok_scales[0, 4 * g : 4 * g + 4, :].bitcast(I32))
+        nc.sync.dma_start(out=qs_raw[:], in_=qs.rearrange("(p j) q -> p j q", j=PACK))
+        nc.sync.dma_start(out=qe_raw[:], in_=qe.rearrange("(p j) q -> p j q", j=PACK))
+        nc.sync.dma_start(start_list[:], offs2)
+        nc.sync.dma_start(end_list[:], offs3)
+
+        warm_in = sb.tile([P, 1], F32, name="warm_in")
+        warm_out = sb.tile([P, 1], F32, name="warm_out")
+        nc.gpsimd.memset(warm_in[:], 0.0)
+        nc.scalar.activation(out=warm_out[:], in_=warm_in[:], func=ACT.Exp)
+
+        def cast(raw, name):
+            grouped = sb.tile([P, Q, PACK], BF16, name=name, align_bytes=64)
+            nc.scalar.copy(out=grouped[:], in_=raw[:].rearrange("p j q -> p q j"))
+            return grouped
+
+        def quantise(grouped, name):
+            codes = sb.tile([P, Q], U32, name=name + "_codes", align_bytes=64)
+            plane = sb.tile([P, Q], U8, name=name + "_scales", align_bytes=64)
+            nc.vector.quantize_mx(out=codes[:].bitcast(FP8X4), scales=plane[:], in_=grouped[:].rearrange("p q j -> p (q j)"))
+            return codes, plane
+
+        picked_words = sb.tile([P, I], U16, name="picked_words", align_bytes=64)
+        picked_scales = sb.tile([P, I], U8, name="picked_scales", align_bytes=64)
+
+        def gather(dst, window, lo, hi):
+            nc.vector.tensor_copy(dst[:, lo:hi], window[:].indirect(tok_list[:, lo // LANES : hi // LANES]))
+
+        def score(query, lo, hi, name):
+            codes, plane = query
+            bank = ps.tile([P, hi - lo], F32, name=name)
+            nc.tensor.matmul_mx(
+                out=bank[:],
+                lhsT=codes[:].bitcast(FP8X4),
+                lhsT_scale=plane[:],
+                rhs=picked_words[:, lo:hi].bitcast(FP4X4),
+                rhs_scale=picked_scales[:, lo:hi],
+                start=True,
+                stop=True,
+            )
+            return bank
+
+        a = sb.tile([P, I], F32, name="a")
+        b = sb.tile([P, I], F32, name="b")
+
+        qs_bf = cast(qs_raw, "qs_bf")
+        qe_bf = cast(qe_raw, "qe_bf")
+
+        gather(picked_words, words, 0, 512)
+        gather(picked_scales, scales, 0, 512)
+        qs_mx = quantise(qs_bf, "qs")
+        gather(picked_words, words, 512, 1024)
+        qe_mx = quantise(qe_bf, "qe")
+        nc.scalar.copy(out=a[:, 0:512], in_=score(qs_mx, 0, 512, "a0")[:])
+        nc.scalar.copy(out=b[:, 0:512], in_=score(qe_mx, 0, 512, "b0")[:])
+        gather(picked_scales, scales, 512, 768)
+        gather(picked_scales, scales, 768, 1024)
+        nc.scalar.copy(out=a[:, 512:768], in_=score(qs_mx, 512, 768, "a1")[:])
+        nc.vector.tensor_copy(out=a[:, 768:1024], in_=score(qs_mx, 768, 1024, "a2")[:])
+        nc.scalar.copy(out=b[:, 512:1024], in_=score(qe_mx, 512, 1024, "b1")[:])
+
+        starts = sb.tile([P, J], F32, name="starts")
+        s = sb.tile([P, J], F32, name="s")
+        nc.vector.tensor_copy(starts[:], a[:].indirect(start_list[:]))
+        nc.vector.tensor_tensor(s[:], b[:].indirect(end_list[:]), starts[:], ALU.add)
+
+        neg_max = sb.tile([P, 1], F32, name="neg_max")
+        total = sb.tile([P, 1], F32, name="total")
+        inv = sb.tile([P, 1], F32, name="inv")
+        p = sb.tile([P, J], F32, name="p")
+        y = sb.tile([P, J], F32, name="y")
+        nc.vector.tensor_reduce(out=neg_max[:], in_=s[:], axis=AX.X, op=ALU.max, negate=True)
+        nc.scalar.activation(out=p[:], in_=s[:], func=ACT.Exp, bias=neg_max[:], accum_out=total[:])
+        nc.vector.reciprocal(out=inv[:], in_=total[:])
+        for h, queue in enumerate((nc.sync, nc.scalar)):
+            cols = slice(h * J // 2, (h + 1) * J // 2)
+            nc.vector.tensor_scalar(out=y[:, cols], in0=p[:, cols], scalar1=inv[:], scalar2=512.0, op0=ALU.mult, op1=ALU.mult)
+            queue.dma_start(out=out[:, cols], in_=y[:, cols])

@@ -33,8 +33,8 @@ def tile_attend_spanpointer_kernel(tc, qs, qe, tok_words, tok_scales, offs, offs
         tok_list = sb.tile([P, I // LANES], U16, name="tok_list")
         start_list = sb.tile([P, J // LANES], U16, name="start_list")
         end_list = sb.tile([P, J // LANES], U16, name="end_list")
-        qs_raw = sb.tile([P, PACK, Q], F32, name="qs_raw")
-        qe_raw = sb.tile([P, PACK, Q], F32, name="qe_raw")
+        qs_raw = sb.tile([P, PACK, Q], F32, name="qs_raw", tag="qs_raw", align_bytes=64)
+        qe_raw = sb.tile([P, PACK, Q], F32, name="qe_raw", tag="qe_raw", align_bytes=64)
 
         nc.vector.memset(scales[:].bitcast(I32), 0)
         nc.sync.dma_start(out=words[:].bitcast(I32), in_=tok_words[0].bitcast(I32))
@@ -52,7 +52,7 @@ def tile_attend_spanpointer_kernel(tc, qs, qe, tok_words, tok_scales, offs, offs
         nc.scalar.activation(out=warm_out[:], in_=warm_in[:], func=ACT.Exp)
 
         def cast(raw, name):
-            grouped = sb.tile([P, Q, PACK], BF16, name=name, align_bytes=64)
+            grouped = sb.tile([P, Q, PACK], BF16, name=name, tag=name, align_bytes=64)
             nc.scalar.copy(out=grouped[:], in_=raw[:].rearrange("p j q -> p q j"))
             return grouped
 
@@ -62,11 +62,11 @@ def tile_attend_spanpointer_kernel(tc, qs, qe, tok_words, tok_scales, offs, offs
             nc.vector.quantize_mx(out=codes[:].bitcast(FP8X4), scales=plane[:], in_=grouped[:].rearrange("p q j -> p (q j)"))
             return codes, plane
 
-        picked_words = sb.tile([P, I], U16, name="picked_words", align_bytes=64)
-        picked_scales = sb.tile([P, I], U8, name="picked_scales", align_bytes=64)
-
         def gather(dst, window, lo, hi):
-            nc.vector.tensor_copy(dst[:, lo:hi], window[:].indirect(tok_list[:, lo // LANES : hi // LANES]))
+            nc.vector.tensor_copy(dst, window[:].indirect(tok_list[:, lo // LANES : hi // LANES]))
+
+        def scale_columns(lo, hi):
+            return scales_first[:, lo:hi] if hi <= 256 else scales_rest[:, lo - 256 : hi - 256]
 
         def score(query, lo, hi, name):
             codes, plane = query
@@ -76,7 +76,7 @@ def tile_attend_spanpointer_kernel(tc, qs, qe, tok_words, tok_scales, offs, offs
                 lhsT=codes[:].bitcast(FP8X4),
                 lhsT_scale=plane[:],
                 rhs=picked_words[:, lo:hi].bitcast(FP4X4),
-                rhs_scale=picked_scales[:, lo:hi],
+                rhs_scale=scale_columns(lo, hi),
                 start=True,
                 stop=True,
             )
@@ -88,23 +88,32 @@ def tile_attend_spanpointer_kernel(tc, qs, qe, tok_words, tok_scales, offs, offs
         qs_bf = cast(qs_raw, "qs_bf")
         qe_bf = cast(qe_raw, "qe_bf")
 
-        gather(picked_words, words, 0, 512)
-        gather(picked_scales, scales, 0, 512)
+        picked_words = sb.tile([P, I], U16, name="picked_words", align_bytes=64)
+        gather(picked_words[:, 0:512], words, 0, 512)
+        gather(picked_words[:, 512:1024], words, 512, 1024)
         qs_mx = quantise(qs_bf, "qs")
-        gather(picked_words, words, 512, 1024)
+        scales_first = sb.tile([P, 256], U8, name="scales_first", tag="qs_raw", align_bytes=64)
+        gather(scale_columns(0, 256), scales, 0, 256)
         qe_mx = quantise(qe_bf, "qe")
-        nc.scalar.copy(out=a[:, 0:512], in_=score(qs_mx, 0, 512, "a0")[:])
-        nc.scalar.copy(out=b[:, 0:512], in_=score(qe_mx, 0, 512, "b0")[:])
-        gather(picked_scales, scales, 512, 768)
-        gather(picked_scales, scales, 768, 1024)
-        nc.scalar.copy(out=a[:, 512:768], in_=score(qs_mx, 512, 768, "a1")[:])
-        nc.vector.tensor_copy(out=a[:, 768:1024], in_=score(qs_mx, 768, 1024, "a2")[:])
-        nc.scalar.copy(out=b[:, 512:1024], in_=score(qe_mx, 512, 1024, "b1")[:])
+        scales_rest = sb.tile([P, 768], U8, name="scales_rest", tag="qe_raw", align_bytes=64)
+        for lo in range(256, 1024, 256):
+            gather(scale_columns(lo, lo + 256), scales, lo, lo + 256)
+        for c in range(3):
+            lo, hi = 256 * c, 256 * (c + 1)
+            nc.scalar.copy(out=a[:, lo:hi], in_=score(qs_mx, lo, hi, "a%d" % c)[:])
+            if c < 2:
+                nc.scalar.copy(out=b[:, lo:hi], in_=score(qe_mx, lo, hi, "b%d" % c)[:])
+        nc.vector.tensor_copy(out=a[:, 768:896], in_=score(qs_mx, 768, 896, "a3")[:])
+        nc.scalar.copy(out=a[:, 896:1024], in_=score(qs_mx, 896, 1024, "a4")[:])
+        nc.scalar.copy(out=b[:, 512:1024], in_=score(qe_mx, 512, 1024, "b2")[:])
 
         starts = sb.tile([P, J], F32, name="starts")
         s = sb.tile([P, J], F32, name="s")
-        nc.vector.tensor_copy(starts[:], a[:].indirect(start_list[:]))
-        nc.vector.tensor_tensor(s[:], b[:].indirect(end_list[:]), starts[:], ALU.add)
+        halves = [(h * J // 2, (h + 1) * J // 2) for h in range(2)]
+        for lo, hi in halves:
+            nc.vector.tensor_copy(starts[:, lo:hi], a[:].indirect(start_list[:, lo // LANES : hi // LANES]))
+        for lo, hi in halves:
+            nc.vector.tensor_tensor(s[:, lo:hi], b[:].indirect(end_list[:, lo // LANES : hi // LANES]), starts[:, lo:hi], ALU.add)
 
         neg_max = sb.tile([P, 1], F32, name="neg_max")
         total = sb.tile([P, 1], F32, name="total")

@@ -39,10 +39,10 @@ def tile_attend_spanpointer_kernel(tc, qs, qe, tok_words, tok_scales, offs, offs
         nc.vector.memset(scales[:].bitcast(I32), 0)
         nc.sync.dma_start(out=words[:].bitcast(I32), in_=tok_words[0].bitcast(I32))
         nc.sync.dma_start(tok_list[:], offs)
-        for g in range(4):
-            nc.sync.dma_start(out=scales[32 * g : 32 * g + 4, :].bitcast(I32), in_=tok_scales[0, 4 * g : 4 * g + 4, :].bitcast(I32))
         nc.sync.dma_start(out=qs_raw[:], in_=qs.rearrange("(p j) q -> p j q", j=PACK))
         nc.sync.dma_start(out=qe_raw[:], in_=qe.rearrange("(p j) q -> p j q", j=PACK))
+        for g in range(4):
+            nc.sync.dma_start(out=scales[32 * g : 32 * g + 4, :].bitcast(I32), in_=tok_scales[0, 4 * g : 4 * g + 4, :].bitcast(I32))
         nc.sync.dma_start(start_list[:], offs2)
         nc.sync.dma_start(end_list[:], offs3)
 
@@ -123,7 +123,7 @@ def tile_attend_spanpointer_kernel(tc, qs, qe, tok_words, tok_scales, offs, offs
         nc.vector.tensor_reduce(out=neg_max[:], in_=s[:], axis=AX.X, op=ALU.max, negate=True)
         nc.scalar.activation(out=p[:], in_=s[:], func=ACT.Exp, bias=neg_max[:], accum_out=total[:])
         nc.vector.reciprocal(out=inv[:], in_=total[:])
-        for h, queue in enumerate((nc.sync, nc.scalar)):
+        for h, queue in enumerate((nc.sync, nc.sync)):
             cols = slice(h * J // 2, (h + 1) * J // 2)
             nc.vector.tensor_scalar(out=y[:, cols], in0=p[:, cols], scalar1=inv[:], scalar2=512.0, op0=ALU.mult, op1=ALU.mult)
             queue.dma_start(out=out[:, cols], in_=y[:, cols])

@@ -28,7 +28,7 @@ def tile_attend_spanpointer_kernel(tc, qs, qe, tok_words, tok_scales, offs, offs
         sb = ctx.enter_context(tc.tile_pool(name="sb", bufs=1))
         ps = ctx.enter_context(tc.psum_pool(name="ps", bufs=1))
 
-        words = sb.tile([P, T], U16, name="words", align_bytes=64)
+        words = sb.tile([P, 2 * T], U16, name="words", align_bytes=64)
         scales = sb.tile([P, T], U8, name="scales", align_bytes=64)
         tok_list = sb.tile([P, I // LANES], U16, name="tok_list")
         start_list = sb.tile([P, J // LANES], U16, name="start_list")
@@ -37,7 +37,8 @@ def tile_attend_spanpointer_kernel(tc, qs, qe, tok_words, tok_scales, offs, offs
         qe_raw = sb.tile([P, PACK, Q], F32, name="qe_raw", tag="qe_raw", align_bytes=64)
 
         nc.vector.memset(scales[:].bitcast(I32), 0)
-        nc.sync.dma_start(out=words[:].bitcast(I32), in_=tok_words[0].bitcast(I32))
+        nc.vector.memset(words[:, T:].bitcast(I32), 0)
+        nc.sync.dma_start(out=words[:, :T].bitcast(I32), in_=tok_words[0].bitcast(I32))
         nc.sync.dma_start(tok_list[:], offs)
         nc.sync.dma_start(out=qs_raw[:], in_=qs.rearrange("(p j) q -> p j q", j=PACK))
         nc.sync.dma_start(out=qe_raw[:], in_=qe.rearrange("(p j) q -> p j q", j=PACK))
@@ -45,11 +46,6 @@ def tile_attend_spanpointer_kernel(tc, qs, qe, tok_words, tok_scales, offs, offs
             nc.sync.dma_start(out=scales[32 * g : 32 * g + 4, :].bitcast(I32), in_=tok_scales[0, 4 * g : 4 * g + 4, :].bitcast(I32))
         nc.sync.dma_start(start_list[:], offs2)
         nc.sync.dma_start(end_list[:], offs3)
-
-        warm_in = sb.tile([P, 1], F32, name="warm_in")
-        warm_out = sb.tile([P, 1], F32, name="warm_out")
-        nc.gpsimd.memset(warm_in[:], 0.0)
-        nc.scalar.activation(out=warm_out[:], in_=warm_in[:], func=ACT.Exp)
 
         def cast(raw, name):
             grouped = sb.tile([P, Q, PACK], BF16, name=name, tag=name, align_bytes=64)
@@ -89,8 +85,7 @@ def tile_attend_spanpointer_kernel(tc, qs, qe, tok_words, tok_scales, offs, offs
         qe_bf = cast(qe_raw, "qe_bf")
 
         picked_words = sb.tile([P, I], U16, name="picked_words", align_bytes=64)
-        gather(picked_words[:, 0:512], words, 0, 512)
-        gather(picked_words[:, 512:1024], words, 512, 1024)
+        gather(picked_words[:], words, 0, I)
         qs_mx = quantise(qs_bf, "qs")
         scales_first = sb.tile([P, 256], U8, name="scales_first", tag="qs_raw", align_bytes=64)
         gather(scale_columns(0, 256), scales, 0, 256)
@@ -105,7 +100,8 @@ def tile_attend_spanpointer_kernel(tc, qs, qe, tok_words, tok_scales, offs, offs
                 nc.scalar.copy(out=b[:, lo:hi], in_=score(qe_mx, lo, hi, "b%d" % c)[:])
         nc.vector.tensor_copy(out=a[:, 768:896], in_=score(qs_mx, 768, 896, "a3")[:])
         nc.scalar.copy(out=a[:, 896:1024], in_=score(qs_mx, 896, 1024, "a4")[:])
-        nc.scalar.copy(out=b[:, 512:1024], in_=score(qe_mx, 512, 1024, "b2")[:])
+        nc.scalar.copy(out=b[:, 512:768], in_=score(qe_mx, 512, 768, "b2")[:])
+        nc.scalar.copy(out=b[:, 768:1024], in_=score(qe_mx, 768, 1024, "a0")[:])
 
         starts = sb.tile([P, J], F32, name="starts")
         s = sb.tile([P, J], F32, name="s")
@@ -123,7 +119,6 @@ def tile_attend_spanpointer_kernel(tc, qs, qe, tok_words, tok_scales, offs, offs
         nc.vector.tensor_reduce(out=neg_max[:], in_=s[:], axis=AX.X, op=ALU.max, negate=True)
         nc.scalar.activation(out=p[:], in_=s[:], func=ACT.Exp, bias=neg_max[:], accum_out=total[:])
         nc.vector.reciprocal(out=inv[:], in_=total[:])
-        for h, queue in enumerate((nc.sync, nc.sync)):
-            cols = slice(h * J // 2, (h + 1) * J // 2)
+        for cols in (slice(0, 192), slice(192, J)):
             nc.vector.tensor_scalar(out=y[:, cols], in0=p[:, cols], scalar1=inv[:], scalar2=512.0, op0=ALU.mult, op1=ALU.mult)
-            queue.dma_start(out=out[:, cols], in_=y[:, cols])
+            nc.sync.dma_start(out=out[:, cols], in_=y[:, cols])

@@ -41,9 +41,9 @@ def tile_attend_spanpointer_kernel(tc, qs, qe, tok_words, tok_scales, offs, offs
         nc.sync.dma_start(out=words[:, :T].bitcast(I32), in_=tok_words[0].bitcast(I32))
         nc.sync.dma_start(tok_list[:], offs)
         nc.sync.dma_start(out=qs_raw[:], in_=qs.rearrange("(p j) q -> p j q", j=PACK))
-        nc.sync.dma_start(out=qe_raw[:], in_=qe.rearrange("(p j) q -> p j q", j=PACK))
         for g in range(4):
-            nc.sync.dma_start(out=scales[32 * g : 32 * g + 4, :].bitcast(I32), in_=tok_scales[0, 4 * g : 4 * g + 4, :].bitcast(I32))
+            nc.sync.dma_start(out=scales[g:P:32, :].bitcast(I32), in_=tok_scales[0, g:16:4, :].bitcast(I32))
+        nc.sync.dma_start(out=qe_raw[:], in_=qe.rearrange("(p j) q -> p j q", j=PACK))
         nc.sync.dma_start(start_list[:], offs2)
         nc.sync.dma_start(end_list[:], offs3)
 
@@ -62,7 +62,7 @@ def tile_attend_spanpointer_kernel(tc, qs, qe, tok_words, tok_scales, offs, offs
             nc.vector.tensor_copy(dst, window[:].indirect(tok_list[:, lo // LANES : hi // LANES]))
 
         def scale_columns(lo, hi):
-            return scales_first[:, lo:hi] if hi <= 256 else scales_rest[:, lo - 256 : hi - 256]
+            return scales_first[:, lo:hi] if hi <= 512 else scales_rest[:, lo - 512 : hi - 512]
 
         def score(query, lo, hi, name):
             codes, plane = query
@@ -87,11 +87,12 @@ def tile_attend_spanpointer_kernel(tc, qs, qe, tok_words, tok_scales, offs, offs
         picked_words = sb.tile([P, I], U16, name="picked_words", align_bytes=64)
         gather(picked_words[:], words, 0, I)
         qs_mx = quantise(qs_bf, "qs")
-        scales_first = sb.tile([P, 256], U8, name="scales_first", tag="qs_raw", align_bytes=64)
-        gather(scale_columns(0, 256), scales, 0, 256)
+        scales_first = sb.tile([P, 512], U8, name="scales_first", tag="qs_raw", align_bytes=64)
+        for lo in range(0, 512, 256):
+            gather(scale_columns(lo, lo + 256), scales, lo, lo + 256)
         qe_mx = quantise(qe_bf, "qe")
-        scales_rest = sb.tile([P, 768], U8, name="scales_rest", tag="qe_raw", align_bytes=64)
-        for lo in range(256, 1024, 256):
+        scales_rest = sb.tile([P, 512], U8, name="scales_rest", tag="qe_raw", align_bytes=64)
+        for lo in range(512, 1024, 256):
             gather(scale_columns(lo, lo + 256), scales, lo, lo + 256)
         for c in range(3):
             lo, hi = 256 * c, 256 * (c + 1)

@@ -28,7 +28,7 @@ def tile_attend_spanpointer_kernel(tc, qs, qe, tok_words, tok_scales, offs, offs
         sb = ctx.enter_context(tc.tile_pool(name="sb", bufs=1))
         ps = ctx.enter_context(tc.psum_pool(name="ps", bufs=1))
 
-        words = sb.tile([P, 2 * T], U16, name="words", align_bytes=64)
+        words = sb.tile([P, T], U16, name="words", align_bytes=64)
         scales = sb.tile([P, T], U8, name="scales", align_bytes=64)
         tok_list = sb.tile([P, I // LANES], U16, name="tok_list")
         start_list = sb.tile([P, J // LANES], U16, name="start_list")
@@ -37,14 +37,13 @@ def tile_attend_spanpointer_kernel(tc, qs, qe, tok_words, tok_scales, offs, offs
         qe_raw = sb.tile([P, PACK, Q], F32, name="qe_raw", tag="qe_raw", align_bytes=64)
 
         nc.vector.memset(scales[:].bitcast(I32), 0)
-        nc.vector.memset(words[:, T:].bitcast(I32), 0)
-        nc.sync.dma_start(out=words[:, :T].bitcast(I32), in_=tok_words[0].bitcast(I32))
         nc.sync.dma_start(tok_list[:], offs)
-        nc.sync.dma_start(out=qs_raw[:], in_=qs.rearrange("(p j) q -> p j q", j=PACK))
+        nc.sync.dma_start(start_list[:], offs2)
         for g in range(4):
             nc.sync.dma_start(out=scales[g:P:32, :].bitcast(I32), in_=tok_scales[0, g:16:4, :].bitcast(I32))
+        nc.sync.dma_start(out=qs_raw[:], in_=qs.rearrange("(p j) q -> p j q", j=PACK))
+        nc.sync.dma_start(out=words[:].bitcast(I32), in_=tok_words[0].bitcast(I32))
         nc.sync.dma_start(out=qe_raw[:], in_=qe.rearrange("(p j) q -> p j q", j=PACK))
-        nc.sync.dma_start(start_list[:], offs2)
         nc.sync.dma_start(end_list[:], offs3)
 
         def cast(raw, name):
@@ -61,8 +60,8 @@ def tile_attend_spanpointer_kernel(tc, qs, qe, tok_words, tok_scales, offs, offs
         def gather(dst, window, lo, hi):
             nc.vector.tensor_copy(dst, window[:].indirect(tok_list[:, lo // LANES : hi // LANES]))
 
-        def scale_columns(lo, hi):
-            return scales_first[:, lo:hi] if hi <= 512 else scales_rest[:, lo - 512 : hi - 512]
+        def word_columns(lo, hi):
+            return words_first[:, lo:hi] if hi <= 512 else words_rest[:, lo - 512 : hi - 512]
 
         def score(query, lo, hi, name):
             codes, plane = query
@@ -71,8 +70,8 @@ def tile_attend_spanpointer_kernel(tc, qs, qe, tok_words, tok_scales, offs, offs
                 out=bank[:],
                 lhsT=codes[:].bitcast(FP8X4),
                 lhsT_scale=plane[:],
-                rhs=picked_words[:, lo:hi].bitcast(FP4X4),
-                rhs_scale=scale_columns(lo, hi),
+                rhs=word_columns(lo, hi).bitcast(FP4X4),
+                rhs_scale=picked_scales[:, lo:hi],
                 start=True,
                 stop=True,
             )
@@ -84,16 +83,16 @@ def tile_attend_spanpointer_kernel(tc, qs, qe, tok_words, tok_scales, offs, offs
         qs_bf = cast(qs_raw, "qs_bf")
         qe_bf = cast(qe_raw, "qe_bf")
 
-        picked_words = sb.tile([P, I], U16, name="picked_words", align_bytes=64)
-        gather(picked_words[:], words, 0, I)
+        picked_scales = sb.tile([P, I], U8, name="picked_scales", align_bytes=64)
+        gather(picked_scales[:], scales, 0, I)
         qs_mx = quantise(qs_bf, "qs")
-        scales_first = sb.tile([P, 512], U8, name="scales_first", tag="qs_raw", align_bytes=64)
+        words_first = sb.tile([P, 512], U16, name="words_first", tag="qs_raw", align_bytes=64)
         for lo in range(0, 512, 256):
-            gather(scale_columns(lo, lo + 256), scales, lo, lo + 256)
+            gather(word_columns(lo, lo + 256), words, lo, lo + 256)
         qe_mx = quantise(qe_bf, "qe")
-        scales_rest = sb.tile([P, 512], U8, name="scales_rest", tag="qe_raw", align_bytes=64)
+        words_rest = sb.tile([P, 512], U16, name="words_rest", tag="qe_raw", align_bytes=64)
         for lo in range(512, 1024, 256):
-            gather(scale_columns(lo, lo + 256), scales, lo, lo + 256)
+            gather(word_columns(lo, lo + 256), words, lo, lo + 256)
         for c in range(3):
             lo, hi = 256 * c, 256 * (c + 1)
             nc.scalar.copy(out=a[:, lo:hi], in_=score(qs_mx, lo, hi, "a%d" % c)[:])

@@ -28,7 +28,7 @@ def tile_attend_spanpointer_kernel(tc, qs, qe, tok_words, tok_scales, offs, offs
         sb = ctx.enter_context(tc.tile_pool(name="sb", bufs=1))
         ps = ctx.enter_context(tc.psum_pool(name="ps", bufs=1))
 
-        words = sb.tile([P, T], U16, name="words", align_bytes=64)
+        words = sb.tile([P, T], U16, name="words", tag="words", align_bytes=64)
         scales = sb.tile([P, T], U8, name="scales", align_bytes=64)
         tok_list = sb.tile([P, I // LANES], U16, name="tok_list")
         start_list = sb.tile([P, J // LANES], U16, name="start_list")
@@ -51,17 +51,14 @@ def tile_attend_spanpointer_kernel(tc, qs, qe, tok_words, tok_scales, offs, offs
             nc.scalar.copy(out=grouped[:], in_=raw[:].rearrange("p j q -> p q j"))
             return grouped
 
-        def quantise(grouped, name):
-            codes = sb.tile([P, Q], U32, name=name + "_codes", align_bytes=64)
+        def quantise(grouped, name, tag):
+            codes = sb.tile([P, Q], U32, name=name + "_codes", tag=tag, align_bytes=64)
             plane = sb.tile([P, Q], U8, name=name + "_scales", align_bytes=64)
             nc.vector.quantize_mx(out=codes[:].bitcast(FP8X4), scales=plane[:], in_=grouped[:].rearrange("p q j -> p (q j)"))
             return codes, plane
 
         def gather(dst, window, lo, hi):
             nc.vector.tensor_copy(dst, window[:].indirect(tok_list[:, lo // LANES : hi // LANES]))
-
-        def word_columns(lo, hi):
-            return words_first[:, lo:hi] if hi <= 512 else words_rest[:, lo - 512 : hi - 512]
 
         def score(query, lo, hi, name):
             codes, plane = query
@@ -70,7 +67,7 @@ def tile_attend_spanpointer_kernel(tc, qs, qe, tok_words, tok_scales, offs, offs
                 out=bank[:],
                 lhsT=codes[:].bitcast(FP8X4),
                 lhsT_scale=plane[:],
-                rhs=word_columns(lo, hi).bitcast(FP4X4),
+                rhs=picked_words[:, lo:hi].bitcast(FP4X4),
                 rhs_scale=picked_scales[:, lo:hi],
                 start=True,
                 stop=True,
@@ -85,23 +82,19 @@ def tile_attend_spanpointer_kernel(tc, qs, qe, tok_words, tok_scales, offs, offs
 
         picked_scales = sb.tile([P, I], U8, name="picked_scales", align_bytes=64)
         gather(picked_scales[:], scales, 0, I)
-        qs_mx = quantise(qs_bf, "qs")
-        words_first = sb.tile([P, 512], U16, name="words_first", tag="qs_raw", align_bytes=64)
-        for lo in range(0, 512, 256):
-            gather(word_columns(lo, lo + 256), words, lo, lo + 256)
-        qe_mx = quantise(qe_bf, "qe")
-        words_rest = sb.tile([P, 512], U16, name="words_rest", tag="qe_raw", align_bytes=64)
-        for lo in range(512, 1024, 256):
-            gather(word_columns(lo, lo + 256), words, lo, lo + 256)
+        qs_mx = quantise(qs_bf, "qs", "qs_codes")
+        picked_words = sb.tile([P, I], U16, name="picked_words", tag="qs_raw", align_bytes=64)
+        for lo in range(0, I, 256):
+            gather(picked_words[:, lo : lo + 256], words, lo, lo + 256)
+        qe_mx = quantise(qe_bf, "qe", "words")
         for c in range(3):
             lo, hi = 256 * c, 256 * (c + 1)
             nc.scalar.copy(out=a[:, lo:hi], in_=score(qs_mx, lo, hi, "a%d" % c)[:])
-            if c < 2:
-                nc.scalar.copy(out=b[:, lo:hi], in_=score(qe_mx, lo, hi, "b%d" % c)[:])
         nc.vector.tensor_copy(out=a[:, 768:896], in_=score(qs_mx, 768, 896, "a3")[:])
         nc.scalar.copy(out=a[:, 896:1024], in_=score(qs_mx, 896, 1024, "a4")[:])
-        nc.scalar.copy(out=b[:, 512:768], in_=score(qe_mx, 512, 768, "b2")[:])
-        nc.scalar.copy(out=b[:, 768:1024], in_=score(qe_mx, 768, 1024, "a0")[:])
+        for c, name in enumerate(("b0", "b1", "b2", "a0")):
+            lo, hi = 256 * c, 256 * (c + 1)
+            nc.scalar.copy(out=b[:, lo:hi], in_=score(qe_mx, lo, hi, name)[:])
 
         starts = sb.tile([P, J], F32, name="starts")
         s = sb.tile([P, J], F32, name="s")

@@ -28,7 +28,7 @@ def tile_attend_spanpointer_kernel(tc, qs, qe, tok_words, tok_scales, offs, offs
         sb = ctx.enter_context(tc.tile_pool(name="sb", bufs=1))
         ps = ctx.enter_context(tc.psum_pool(name="ps", bufs=1))
 
-        words = sb.tile([P, T], U16, name="words", tag="words", align_bytes=64)
+        words = sb.tile([P, T], U16, name="words", align_bytes=64)
         scales = sb.tile([P, T], U8, name="scales", align_bytes=64)
         tok_list = sb.tile([P, I // LANES], U16, name="tok_list")
         start_list = sb.tile([P, J // LANES], U16, name="start_list")
@@ -51,8 +51,8 @@ def tile_attend_spanpointer_kernel(tc, qs, qe, tok_words, tok_scales, offs, offs
             nc.scalar.copy(out=grouped[:], in_=raw[:].rearrange("p j q -> p q j"))
             return grouped
 
-        def quantise(grouped, name, tag):
-            codes = sb.tile([P, Q], U32, name=name + "_codes", tag=tag, align_bytes=64)
+        def quantise(grouped, name):
+            codes = sb.tile([P, Q], U32, name=name + "_codes", align_bytes=64)
             plane = sb.tile([P, Q], U8, name=name + "_scales", align_bytes=64)
             nc.vector.quantize_mx(out=codes[:].bitcast(FP8X4), scales=plane[:], in_=grouped[:].rearrange("p q j -> p (q j)"))
             return codes, plane
@@ -82,11 +82,11 @@ def tile_attend_spanpointer_kernel(tc, qs, qe, tok_words, tok_scales, offs, offs
 
         picked_scales = sb.tile([P, I], U8, name="picked_scales", align_bytes=64)
         gather(picked_scales[:], scales, 0, I)
-        qs_mx = quantise(qs_bf, "qs", "qs_codes")
+        qs_mx = quantise(qs_bf, "qs")
         picked_words = sb.tile([P, I], U16, name="picked_words", tag="qs_raw", align_bytes=64)
-        for lo in range(0, I, 256):
-            gather(picked_words[:, lo : lo + 256], words, lo, lo + 256)
-        qe_mx = quantise(qe_bf, "qe", "words")
+        for lo, hi in ((0, 512), (512, 768), (768, I)):
+            gather(picked_words[:, lo:hi], words, lo, hi)
+        qe_mx = quantise(qe_bf, "qe")
         for c in range(3):
             lo, hi = 256 * c, 256 * (c + 1)
             nc.scalar.copy(out=a[:, lo:hi], in_=score(qs_mx, lo, hi, "a%d" % c)[:])

@@ -40,11 +40,12 @@ def tile_attend_spanpointer_kernel(tc, qs, qe, tok_words, tok_scales, offs, offs
         nc.sync.dma_start(tok_list[:], offs)
         nc.sync.dma_start(start_list[:], offs2)
         for g in range(4):
-            nc.sync.dma_start(out=scales[g:P:32, :].bitcast(I32), in_=tok_scales[0, g:16:4, :].bitcast(I32))
-        nc.sync.dma_start(out=qs_raw[:], in_=qs.rearrange("(p j) q -> p j q", j=PACK))
-        nc.sync.dma_start(out=words[:].bitcast(I32), in_=tok_words[0].bitcast(I32))
-        nc.sync.dma_start(out=qe_raw[:], in_=qe.rearrange("(p j) q -> p j q", j=PACK))
+            queue = nc.sync if g < 2 else nc.scalar
+            queue.dma_start(out=scales[g:P:32, :].bitcast(I32), in_=tok_scales[0, g:16:4, :].bitcast(I32))
         nc.sync.dma_start(end_list[:], offs3)
+        nc.sync.dma_start(out=words[:].bitcast(I32), in_=tok_words[0].bitcast(I32))
+        nc.sync.dma_start(out=qs_raw[:], in_=qs.rearrange("(p j) q -> p j q", j=PACK))
+        nc.sync.dma_start(out=qe_raw[:], in_=qe.rearrange("(p j) q -> p j q", j=PACK))
 
         def cast(raw, name):
             grouped = sb.tile([P, Q, PACK], BF16, name=name, tag=name, align_bytes=64)
@@ -60,6 +61,9 @@ def tile_attend_spanpointer_kernel(tc, qs, qe, tok_words, tok_scales, offs, offs
         def gather(dst, window, lo, hi):
             nc.vector.tensor_copy(dst, window[:].indirect(tok_list[:, lo // LANES : hi // LANES]))
 
+        def word_columns(lo, hi):
+            return words_first[:, lo:hi] if hi <= 512 else words_rest[:, lo - 512 : hi - 512]
+
         def score(query, lo, hi, name):
             codes, plane = query
             bank = ps.tile([P, hi - lo], F32, name=name)
@@ -67,7 +71,7 @@ def tile_attend_spanpointer_kernel(tc, qs, qe, tok_words, tok_scales, offs, offs
                 out=bank[:],
                 lhsT=codes[:].bitcast(FP8X4),
                 lhsT_scale=plane[:],
-                rhs=picked_words[:, lo:hi].bitcast(FP4X4),
+                rhs=word_columns(lo, hi).bitcast(FP4X4),
                 rhs_scale=picked_scales[:, lo:hi],
                 start=True,
                 stop=True,
@@ -82,10 +86,12 @@ def tile_attend_spanpointer_kernel(tc, qs, qe, tok_words, tok_scales, offs, offs
 
         picked_scales = sb.tile([P, I], U8, name="picked_scales", align_bytes=64)
         gather(picked_scales[:], scales, 0, I)
+        words_first = sb.tile([P, 512], U16, name="words_first", align_bytes=64)
+        gather(words_first[:], words, 0, 512)
         qs_mx = quantise(qs_bf, "qs")
-        picked_words = sb.tile([P, I], U16, name="picked_words", tag="qs_raw", align_bytes=64)
-        for lo, hi in ((0, 512), (512, 768), (768, I)):
-            gather(picked_words[:, lo:hi], words, lo, hi)
+        words_rest = sb.tile([P, 512], U16, name="words_rest", tag="qs_raw", align_bytes=64)
+        for lo in range(512, I, 256):
+            gather(word_columns(lo, lo + 256), words, lo, lo + 256)
         qe_mx = quantise(qe_bf, "qe")
         for c in range(3):
             lo, hi = 256 * c, 256 * (c + 1)

@@ -36,16 +36,22 @@ def tile_attend_spanpointer_kernel(tc, qs, qe, tok_words, tok_scales, offs, offs
         qs_raw = sb.tile([P, PACK, Q], F32, name="qs_raw", tag="qs_raw", align_bytes=64)
         qe_raw = sb.tile([P, PACK, Q], F32, name="qe_raw", tag="qe_raw", align_bytes=64)
 
-        nc.vector.memset(scales[:].bitcast(I32), 0)
+        def load_scales(queue, g, lo, hi):
+            queue.dma_start(out=scales[g:P:32, lo:hi].bitcast(I32), in_=tok_scales[0, g:16:4, lo:hi].bitcast(I32))
+
+        nc.vector.memset(scales[:, : T // 2].bitcast(I32), 0)
+        nc.vector.memset(scales[:, T // 2 :].bitcast(I32), 0)
         nc.sync.dma_start(tok_list[:], offs)
-        nc.sync.dma_start(start_list[:], offs2)
-        for g in range(4):
-            queue = nc.sync if g < 2 else nc.scalar
-            queue.dma_start(out=scales[g:P:32, :].bitcast(I32), in_=tok_scales[0, g:16:4, :].bitcast(I32))
-        nc.sync.dma_start(end_list[:], offs3)
+        for lo, hi in ((0, T // 2), (T // 2, T)):
+            load_scales(nc.sync, 0, lo, hi)
+            load_scales(nc.scalar, 1, lo, hi)
+        load_scales(nc.sync, 2, 0, T)
+        load_scales(nc.sync, 3, 0, T)
         nc.sync.dma_start(out=words[:].bitcast(I32), in_=tok_words[0].bitcast(I32))
         nc.sync.dma_start(out=qs_raw[:], in_=qs.rearrange("(p j) q -> p j q", j=PACK))
         nc.sync.dma_start(out=qe_raw[:], in_=qe.rearrange("(p j) q -> p j q", j=PACK))
+        nc.sync.dma_start(start_list[:], offs2)
+        nc.sync.dma_start(end_list[:], offs3)
 
         def cast(raw, name):
             grouped = sb.tile([P, Q, PACK], BF16, name=name, tag=name, align_bytes=64)

@@ -42,15 +42,15 @@ def tile_attend_spanpointer_kernel(tc, qs, qe, tok_words, tok_scales, offs, offs
         nc.vector.memset(scales[:, : T // 2].bitcast(I32), 0)
         nc.vector.memset(scales[:, T // 2 :].bitcast(I32), 0)
         nc.sync.dma_start(tok_list[:], offs)
-        for lo, hi in ((0, T // 2), (T // 2, T)):
-            load_scales(nc.sync, 0, lo, hi)
-            load_scales(nc.scalar, 1, lo, hi)
+        load_scales(nc.sync, 0, 0, T // 2)
+        load_scales(nc.scalar, 1, 0, T)
+        load_scales(nc.sync, 0, T // 2, T)
         load_scales(nc.sync, 2, 0, T)
         load_scales(nc.sync, 3, 0, T)
+        nc.sync.dma_start(start_list[:], offs2)
         nc.sync.dma_start(out=words[:].bitcast(I32), in_=tok_words[0].bitcast(I32))
         nc.sync.dma_start(out=qs_raw[:], in_=qs.rearrange("(p j) q -> p j q", j=PACK))
         nc.sync.dma_start(out=qe_raw[:], in_=qe.rearrange("(p j) q -> p j q", j=PACK))
-        nc.sync.dma_start(start_list[:], offs2)
         nc.sync.dma_start(end_list[:], offs3)
 
         def cast(raw, name):

@@ -20,6 +20,7 @@ AX = mybir.AxisListType
 P = 128
 PACK = 4
 LANES = 16
+QUARTER = I // 4
 
 
 def tile_attend_spanpointer_kernel(tc, qs, qe, tok_words, tok_scales, offs, offs2, offs3, out):
@@ -67,17 +68,24 @@ def tile_attend_spanpointer_kernel(tc, qs, qe, tok_words, tok_scales, offs, offs
         def gather(dst, window, lo, hi):
             nc.vector.tensor_copy(dst, window[:].indirect(tok_list[:, lo // LANES : hi // LANES]))
 
-        def word_columns(lo, hi):
-            return words_first[:, lo:hi] if hi <= 512 else words_rest[:, lo - 512 : hi - 512]
+        picked_words = []
 
-        def score(query, lo, hi, name):
+        def gather_words(tag, quarters):
+            piece = sb.tile([P, quarters, QUARTER], U16, name="picked_" + tag, tag=tag, align_bytes=64)
+            for k in range(quarters):
+                c = len(picked_words)
+                gather(piece[:, k, :], words, c * QUARTER, (c + 1) * QUARTER)
+                picked_words.append(piece[:, k, :])
+
+        def score(query, lo, hi, bank_name):
             codes, plane = query
-            bank = ps.tile([P, hi - lo], F32, name=name)
+            bank = ps.tile([P, hi - lo], F32, name=bank_name)
+            c = lo // QUARTER
             nc.tensor.matmul_mx(
                 out=bank[:],
                 lhsT=codes[:].bitcast(FP8X4),
                 lhsT_scale=plane[:],
-                rhs=word_columns(lo, hi).bitcast(FP4X4),
+                rhs=picked_words[c][:, lo - c * QUARTER : hi - c * QUARTER].bitcast(FP4X4),
                 rhs_scale=picked_scales[:, lo:hi],
                 start=True,
                 stop=True,
@@ -92,37 +100,53 @@ def tile_attend_spanpointer_kernel(tc, qs, qe, tok_words, tok_scales, offs, offs
 
         picked_scales = sb.tile([P, I], U8, name="picked_scales", align_bytes=64)
         gather(picked_scales[:], scales, 0, I)
-        words_first = sb.tile([P, 512], U16, name="words_first", align_bytes=64)
-        gather(words_first[:], words, 0, 512)
+        gather_words("words_first", 1)
         qs_mx = quantise(qs_bf, "qs")
-        words_rest = sb.tile([P, 512], U16, name="words_rest", tag="qs_raw", align_bytes=64)
-        for lo in range(512, I, 256):
-            gather(word_columns(lo, lo + 256), words, lo, lo + 256)
+        gather_words("qs_raw", 1)
         qe_mx = quantise(qe_bf, "qe")
-        for c in range(3):
-            lo, hi = 256 * c, 256 * (c + 1)
-            nc.scalar.copy(out=a[:, lo:hi], in_=score(qs_mx, lo, hi, "a%d" % c)[:])
-        nc.vector.tensor_copy(out=a[:, 768:896], in_=score(qs_mx, 768, 896, "a3")[:])
-        nc.scalar.copy(out=a[:, 896:1024], in_=score(qs_mx, 896, 1024, "a4")[:])
-        for c, name in enumerate(("b0", "b1", "b2", "a0")):
-            lo, hi = 256 * c, 256 * (c + 1)
-            nc.scalar.copy(out=b[:, lo:hi], in_=score(qe_mx, lo, hi, name)[:])
+        gather_words("qe_raw", 2)
+
+        def by_scalar(dst, query, lo, hi, bank_name):
+            nc.scalar.copy(out=dst[:, lo:hi], in_=score(query, lo, hi, bank_name)[:])
+
+        def by_vector(dst, query, lo, hi, bank_name):
+            nc.vector.tensor_copy(out=dst[:, lo:hi], in_=score(query, lo, hi, bank_name)[:])
+
+        by_scalar(a, qs_mx, 0, 256, "bank0")
+        by_scalar(a, qs_mx, 256, 512, "bank1")
+        by_scalar(b, qe_mx, 0, 256, "bank2")
+        by_scalar(b, qe_mx, 256, 512, "bank3")
+        by_scalar(b, qe_mx, 512, 768, "bank4")
+        by_vector(a, qs_mx, 512, 768, "bank5")
+        by_scalar(b, qe_mx, 768, 896, "bank6")
+        by_vector(b, qe_mx, 896, 1024, "bank7")
+        by_scalar(a, qs_mx, 768, 896, "bank0")
+        by_scalar(a, qs_mx, 896, 1024, "bank1")
 
         starts = sb.tile([P, J], F32, name="starts")
-        s = sb.tile([P, J], F32, name="s")
-        halves = [(h * J // 2, (h + 1) * J // 2) for h in range(2)]
-        for lo, hi in halves:
-            nc.vector.tensor_copy(starts[:, lo:hi], a[:].indirect(start_list[:, lo // LANES : hi // LANES]))
-        for lo, hi in halves:
-            nc.vector.tensor_tensor(s[:, lo:hi], b[:].indirect(end_list[:, lo // LANES : hi // LANES]), starts[:, lo:hi], ALU.add)
-
+        ends = sb.tile([P, J], F32, name="ends")
+        s = sb.tile([P, J + 2], F32, name="s")
         neg_max = sb.tile([P, 1], F32, name="neg_max")
+
+        def offsets(spans, lo, hi):
+            return spans[:, lo // LANES : hi // LANES]
+
+        for lo in range(0, J, 128):
+            nc.scalar.activation(starts[:, lo : lo + 128], a[:].indirect(offsets(start_list, lo, lo + 128)), ACT.Copy)
+        nc.vector.tensor_copy(ends[:, 128:J], b[:].indirect(offsets(end_list, 128, J)))
+        nc.vector.tensor_tensor(s[:, 0:128], b[:].indirect(offsets(end_list, 0, 128)), starts[:, 0:128], ALU.add)
+        nc.vector.tensor_tensor(s[:, 128:256], ends[:, 128:256], starts[:, 128:256], ALU.add)
+        nc.vector.tensor_reduce(out=s[:, J : J + 1], in_=s[:, 0:128], axis=AX.X, op=ALU.max)
+        nc.vector.tensor_tensor(s[:, 256:384], ends[:, 256:384], starts[:, 256:384], ALU.add)
+        nc.vector.tensor_reduce(out=s[:, J + 1 : J + 2], in_=s[:, 128:256], axis=AX.X, op=ALU.max)
+        nc.vector.tensor_tensor(s[:, 384:J], ends[:, 384:J], starts[:, 384:J], ALU.add)
+        nc.vector.tensor_reduce(out=neg_max[:], in_=s[:, 256 : J + 2], axis=AX.X, op=ALU.max, negate=True)
+
         total = sb.tile([P, 1], F32, name="total")
         inv = sb.tile([P, 1], F32, name="inv")
         p = sb.tile([P, J], F32, name="p")
         y = sb.tile([P, J], F32, name="y")
-        nc.vector.tensor_reduce(out=neg_max[:], in_=s[:], axis=AX.X, op=ALU.max, negate=True)
-        nc.scalar.activation(out=p[:], in_=s[:], func=ACT.Exp, bias=neg_max[:], accum_out=total[:])
+        nc.scalar.activation(out=p[:], in_=s[:, :J], func=ACT.Exp, bias=neg_max[:], accum_out=total[:])
         nc.vector.reciprocal(out=inv[:], in_=total[:])
         for cols in (slice(0, 192), slice(192, J)):
             nc.vector.tensor_scalar(out=y[:, cols], in0=p[:, cols], scalar1=inv[:], scalar2=512.0, op0=ALU.mult, op1=ALU.mult)

@@ -44,15 +44,14 @@ def tile_attend_spanpointer_kernel(tc, qs, qe, tok_words, tok_scales, offs, offs
         nc.vector.memset(scales[:, T // 2 :].bitcast(I32), 0)
         nc.sync.dma_start(tok_list[:], offs)
         load_scales(nc.sync, 0, 0, T // 2)
-        load_scales(nc.scalar, 1, 0, T)
         load_scales(nc.sync, 0, T // 2, T)
-        load_scales(nc.sync, 2, 0, T)
-        load_scales(nc.sync, 3, 0, T)
-        nc.sync.dma_start(start_list[:], offs2)
-        nc.sync.dma_start(out=words[:].bitcast(I32), in_=tok_words[0].bitcast(I32))
+        for g in range(1, 4):
+            load_scales(nc.sync, g, 0, T)
         nc.sync.dma_start(out=qs_raw[:], in_=qs.rearrange("(p j) q -> p j q", j=PACK))
+        nc.sync.dma_start(out=words[:].bitcast(I32), in_=tok_words[0].bitcast(I32))
         nc.sync.dma_start(out=qe_raw[:], in_=qe.rearrange("(p j) q -> p j q", j=PACK))
         nc.sync.dma_start(end_list[:], offs3)
+        nc.sync.dma_start(start_list[:], offs2)
 
         def cast(raw, name):
             grouped = sb.tile([P, Q, PACK], BF16, name=name, tag=name, align_bytes=64)

@@ -55,7 +55,10 @@ def tile_attend_spanpointer_kernel(tc, qs, qe, tok_words, tok_scales, offs, offs
 
         def cast(raw, name):
             grouped = sb.tile([P, Q, PACK], BF16, name=name, tag=name, align_bytes=64)
-            nc.scalar.copy(out=grouped[:], in_=raw[:].rearrange("p j q -> p q j"))
+            nc.scalar.copy(
+                out=grouped[:].rearrange("p (c i) j -> p c j i", i=4),
+                in_=raw[:].rearrange("p j (c i) -> p c j i", i=4),
+            )
             return grouped
 
         def quantise(grouped, name):

@@ -118,31 +118,35 @@ def tile_attend_spanpointer_kernel(tc, qs, qe, tok_words, tok_scales, offs, offs
         by_scalar(a, qs_mx, 256, 512, "bank1")
         by_scalar(b, qe_mx, 0, 256, "bank2")
         by_scalar(b, qe_mx, 256, 512, "bank3")
-        by_scalar(b, qe_mx, 512, 768, "bank4")
-        by_vector(a, qs_mx, 512, 768, "bank5")
-        by_scalar(b, qe_mx, 768, 896, "bank6")
-        by_vector(b, qe_mx, 896, 1024, "bank7")
-        by_scalar(a, qs_mx, 768, 896, "bank0")
-        by_scalar(a, qs_mx, 896, 1024, "bank1")
+        by_scalar(a, qs_mx, 512, 768, "bank4")
+        by_vector(b, qe_mx, 512, 768, "bank5")
+        by_scalar(a, qs_mx, 768, 896, "bank6")
+        by_scalar(a, qs_mx, 896, 1024, "bank7")
+        by_vector(b, qe_mx, 768, 896, "bank0")
+        by_vector(b, qe_mx, 896, 1024, "bank1")
 
-        starts = sb.tile([P, J], F32, name="starts")
-        ends = sb.tile([P, J], F32, name="ends")
-        s = sb.tile([P, J + 2], F32, name="s")
+        s = sb.tile([P, J + 1], F32, name="s")
         neg_max = sb.tile([P, 1], F32, name="neg_max")
 
         def offsets(spans, lo, hi):
             return spans[:, lo // LANES : hi // LANES]
 
-        for lo in range(0, J, 128):
-            nc.scalar.activation(starts[:, lo : lo + 128], a[:].indirect(offsets(start_list, lo, lo + 128)), ACT.Copy)
-        nc.vector.tensor_copy(ends[:, 128:J], b[:].indirect(offsets(end_list, 128, J)))
-        nc.vector.tensor_tensor(s[:, 0:128], b[:].indirect(offsets(end_list, 0, 128)), starts[:, 0:128], ALU.add)
-        nc.vector.tensor_tensor(s[:, 128:256], ends[:, 128:256], starts[:, 128:256], ALU.add)
-        nc.vector.tensor_reduce(out=s[:, J : J + 1], in_=s[:, 0:128], axis=AX.X, op=ALU.max)
-        nc.vector.tensor_tensor(s[:, 256:384], ends[:, 256:384], starts[:, 256:384], ALU.add)
-        nc.vector.tensor_reduce(out=s[:, J + 1 : J + 2], in_=s[:, 128:256], axis=AX.X, op=ALU.max)
-        nc.vector.tensor_tensor(s[:, 384:J], ends[:, 384:J], starts[:, 384:J], ALU.add)
-        nc.vector.tensor_reduce(out=neg_max[:], in_=s[:, 256 : J + 2], axis=AX.X, op=ALU.max, negate=True)
+        def starts_by_scalar(lo, hi, tag):
+            piece = sb.tile([P, hi - lo], F32, name="starts%d" % lo, tag=tag)
+            nc.scalar.activation(piece[:], a[:].indirect(offsets(start_list, lo, hi)), ACT.Copy)
+            return piece
+
+        cuts = [(0, 64), (64, 224), (224, 384)]
+        starts = [starts_by_scalar(lo, hi, "spans%d" % lo) for lo, hi in cuts]
+        last_starts = sb.tile([P, 128], F32, name="last_starts")
+        nc.vector.tensor_copy(last_starts[:], a[:].indirect(offsets(start_list, 384, J)))
+        for (lo, hi), piece in zip(cuts, starts):
+            nc.vector.tensor_tensor(s[:, lo:hi], b[:].indirect(offsets(end_list, lo, hi)), piece[:], ALU.add)
+        last_ends = sb.tile([P, 128], F32, name="last_ends", tag="spans0")
+        nc.scalar.activation(last_ends[:], b[:].indirect(offsets(end_list, 384, J)), ACT.Copy)
+        nc.vector.tensor_reduce(out=s[:, J : J + 1], in_=s[:, 0:224], axis=AX.X, op=ALU.max)
+        nc.vector.tensor_tensor(s[:, 384:J], last_ends[:], last_starts[:], ALU.add)
+        nc.vector.tensor_reduce(out=neg_max[:], in_=s[:, 224 : J + 1], axis=AX.X, op=ALU.max, negate=True)
 
         total = sb.tile([P, 1], F32, name="total")
         inv = sb.tile([P, 1], F32, name="inv")

@@ -44,9 +44,10 @@ def tile_attend_spanpointer_kernel(tc, qs, qe, tok_words, tok_scales, offs, offs
         nc.vector.memset(scales[:, T // 2 :].bitcast(I32), 0)
         nc.sync.dma_start(tok_list[:], offs)
         load_scales(nc.sync, 0, 0, T // 2)
+        load_scales(nc.scalar, 1, 0, T)
         load_scales(nc.sync, 0, T // 2, T)
-        for g in range(1, 4):
-            load_scales(nc.sync, g, 0, T)
+        load_scales(nc.sync, 2, 0, T)
+        load_scales(nc.sync, 3, 0, T)
         nc.sync.dma_start(out=qs_raw[:], in_=qs.rearrange("(p j) q -> p j q", j=PACK))
         nc.sync.dma_start(out=words[:].bitcast(I32), in_=tok_words[0].bitcast(I32))
         nc.sync.dma_start(out=qe_raw[:], in_=qe.rearrange("(p j) q -> p j q", j=PACK))

@@ -45,9 +45,9 @@ def tile_attend_spanpointer_kernel(tc, qs, qe, tok_words, tok_scales, offs, offs
         nc.sync.dma_start(tok_list[:], offs)
         load_scales(nc.sync, 0, 0, T // 2)
         load_scales(nc.scalar, 1, 0, T)
-        load_scales(nc.sync, 0, T // 2, T)
         load_scales(nc.sync, 2, 0, T)
         load_scales(nc.sync, 3, 0, T)
+        load_scales(nc.sync, 0, T // 2, T)
         nc.sync.dma_start(out=qs_raw[:], in_=qs.rearrange("(p j) q -> p j q", j=PACK))
         nc.sync.dma_start(out=words[:].bitcast(I32), in_=tok_words[0].bitcast(I32))
         nc.sync.dma_start(out=qe_raw[:], in_=qe.rearrange("(p j) q -> p j q", j=PACK))

@@ -128,26 +128,27 @@ def tile_attend_spanpointer_kernel(tc, qs, qe, tok_words, tok_scales, offs, offs
 
         s = sb.tile([P, J + 1], F32, name="s")
         neg_max = sb.tile([P, 1], F32, name="neg_max")
+        first_starts = sb.tile([P, 64], F32, name="first_starts", tag="first_then_last")
+        starts = sb.tile([P, J], F32, name="starts")
 
         def offsets(spans, lo, hi):
             return spans[:, lo // LANES : hi // LANES]
 
-        def starts_by_scalar(lo, hi, tag):
-            piece = sb.tile([P, hi - lo], F32, name="starts%d" % lo, tag=tag)
-            nc.scalar.activation(piece[:], a[:].indirect(offsets(start_list, lo, hi)), ACT.Copy)
-            return piece
+        def look_up_and_add(lo, hi, known):
+            nc.vector.tensor_tensor(s[:, lo:hi], b[:].indirect(offsets(end_list, lo, hi)), known, ALU.add)
 
-        cuts = [(0, 64), (64, 224), (224, 384)]
-        starts = [starts_by_scalar(lo, hi, "spans%d" % lo) for lo, hi in cuts]
-        last_starts = sb.tile([P, 128], F32, name="last_starts")
-        nc.vector.tensor_copy(last_starts[:], a[:].indirect(offsets(start_list, 384, J)))
-        for (lo, hi), piece in zip(cuts, starts):
-            nc.vector.tensor_tensor(s[:, lo:hi], b[:].indirect(offsets(end_list, lo, hi)), piece[:], ALU.add)
-        last_ends = sb.tile([P, 128], F32, name="last_ends", tag="spans0")
-        nc.scalar.activation(last_ends[:], b[:].indirect(offsets(end_list, 384, J)), ACT.Copy)
-        nc.vector.tensor_reduce(out=s[:, J : J + 1], in_=s[:, 0:224], axis=AX.X, op=ALU.max)
-        nc.vector.tensor_tensor(s[:, 384:J], last_ends[:], last_starts[:], ALU.add)
-        nc.vector.tensor_reduce(out=neg_max[:], in_=s[:, 224 : J + 1], axis=AX.X, op=ALU.max, negate=True)
+        nc.scalar.activation(first_starts[:], a[:].indirect(offsets(start_list, 0, 64)), ACT.Copy)
+        for lo, hi in ((64, 192), (192, 352)):
+            nc.scalar.activation(starts[:, lo:hi], a[:].indirect(offsets(start_list, lo, hi)), ACT.Copy)
+        nc.vector.tensor_copy(starts[:, 352:J], a[:].indirect(offsets(start_list, 352, J)))
+        look_up_and_add(0, 64, first_starts[:])
+        look_up_and_add(64, 192, starts[:, 64:192])
+        look_up_and_add(192, 320, starts[:, 192:320])
+        last_ends = sb.tile([P, J - 320], F32, name="last_ends", tag="first_then_last")
+        nc.scalar.activation(last_ends[:], b[:].indirect(offsets(end_list, 320, J)), ACT.Copy)
+        nc.vector.tensor_reduce(out=s[:, J : J + 1], in_=s[:, 0:192], axis=AX.X, op=ALU.max)
+        nc.vector.tensor_tensor(s[:, 320:J], last_ends[:], starts[:, 320:J], ALU.add)
+        nc.vector.tensor_reduce(out=neg_max[:], in_=s[:, 192 : J + 1], axis=AX.X, op=ALU.max, negate=True)
 
         total = sb.tile([P, 1], F32, name="total")
         inv = sb.tile([P, 1], F32, name="inv")

@@ -110,10 +110,10 @@ def tile_attend_spanpointer_kernel(tc, qs, qe, tok_words, tok_scales, offs, offs
         gather_words("qe_raw", 2)
 
         def by_scalar(dst, query, lo, hi, bank_name):
-            nc.scalar.copy(out=dst[:, lo:hi], in_=score(query, lo, hi, bank_name)[:])
+            nc.scalar.activation(out=dst[:, lo:hi], in_=score(query, lo, hi, bank_name)[:], func=ACT.Copy, scale=-1.0)
 
         def by_vector(dst, query, lo, hi, bank_name):
-            nc.vector.tensor_copy(out=dst[:, lo:hi], in_=score(query, lo, hi, bank_name)[:])
+            nc.vector.tensor_scalar(out=dst[:, lo:hi], in0=score(query, lo, hi, bank_name)[:], scalar1=-1.0, scalar2=None, op0=ALU.mult)
 
         by_scalar(a, qs_mx, 0, 256, "bank0")
         by_scalar(a, qs_mx, 256, 512, "bank1")
@@ -126,9 +126,12 @@ def tile_attend_spanpointer_kernel(tc, qs, qe, tok_words, tok_scales, offs, offs
         by_vector(b, qe_mx, 768, 896, "bank0")
         by_vector(b, qe_mx, 896, 1024, "bank1")
 
+        OWN, FIRST, EARLY, FILL = 160, 224, 320, 384
+        LATE = J - EARLY
         s = sb.tile([P, J + 1], F32, name="s")
+        neg_early = s[:, J : J + 1]
         neg_max = sb.tile([P, 1], F32, name="neg_max")
-        first_starts = sb.tile([P, 64], F32, name="first_starts", tag="first_then_last")
+        first_starts = sb.tile([P, FIRST - OWN], F32, name="first_starts", tag="first_then_last")
         starts = sb.tile([P, J], F32, name="starts")
 
         def offsets(spans, lo, hi):
@@ -137,25 +140,37 @@ def tile_attend_spanpointer_kernel(tc, qs, qe, tok_words, tok_scales, offs, offs
         def look_up_and_add(lo, hi, known):
             nc.vector.tensor_tensor(s[:, lo:hi], b[:].indirect(offsets(end_list, lo, hi)), known, ALU.add)
 
-        nc.scalar.activation(first_starts[:], a[:].indirect(offsets(start_list, 0, 64)), ACT.Copy)
-        for lo, hi in ((64, 192), (192, 352)):
+        nc.scalar.activation(first_starts[:], a[:].indirect(offsets(start_list, OWN, FIRST)), ACT.Copy)
+        for lo, hi in ((FIRST, EARLY), (EARLY, J)):
             nc.scalar.activation(starts[:, lo:hi], a[:].indirect(offsets(start_list, lo, hi)), ACT.Copy)
-        nc.vector.tensor_copy(starts[:, 352:J], a[:].indirect(offsets(start_list, 352, J)))
-        look_up_and_add(0, 64, first_starts[:])
-        look_up_and_add(64, 192, starts[:, 64:192])
-        look_up_and_add(192, 320, starts[:, 192:320])
-        last_ends = sb.tile([P, J - 320], F32, name="last_ends", tag="first_then_last")
-        nc.scalar.activation(last_ends[:], b[:].indirect(offsets(end_list, 320, J)), ACT.Copy)
-        nc.vector.tensor_reduce(out=s[:, J : J + 1], in_=s[:, 0:192], axis=AX.X, op=ALU.max)
-        nc.vector.tensor_tensor(s[:, 320:J], last_ends[:], starts[:, 320:J], ALU.add)
-        nc.vector.tensor_reduce(out=neg_max[:], in_=s[:, 192 : J + 1], axis=AX.X, op=ALU.max, negate=True)
+        nc.vector.tensor_copy(starts[:, :OWN], a[:].indirect(offsets(start_list, 0, OWN)))
+        look_up_and_add(OWN, FIRST, first_starts[:])
+        look_up_and_add(0, OWN, starts[:, :OWN])
+        look_up_and_add(FIRST, EARLY, starts[:, FIRST:EARLY])
+        look_up_and_add(EARLY, FILL, starts[:, EARLY:FILL])
+        last_ends = sb.tile([P, J - FILL], F32, name="last_ends", tag="first_then_last")
+        nc.scalar.activation(last_ends[:], b[:].indirect(offsets(end_list, FILL, J)), ACT.Copy)
+        nc.vector.tensor_reduce(out=neg_early, in_=s[:, :EARLY], axis=AX.X, op=ALU.min)
+        nc.vector.tensor_tensor(s[:, FILL:J], last_ends[:], starts[:, FILL:J], ALU.add)
+        nc.vector.tensor_reduce(out=neg_max[:], in_=s[:, EARLY:], axis=AX.X, op=ALU.min)
 
+        early_sum = sb.tile([P, 1], F32, name="early_sum")
+        early_rest = sb.tile([P, 1], F32, name="early_rest")
+        late_sum = sb.tile([P, 1], F32, name="late_sum")
         total = sb.tile([P, 1], F32, name="total")
+        early_gain = sb.tile([P, 1], F32, name="early_gain")
         inv = sb.tile([P, 1], F32, name="inv")
-        p = sb.tile([P, J], F32, name="p")
+        p_early = sb.tile([P, EARLY], F32, name="p_early")
+        p_late = sb.tile([P, LATE + 1], F32, name="p_late")
         y = sb.tile([P, J], F32, name="y")
-        nc.scalar.activation(out=p[:], in_=s[:, :J], func=ACT.Exp, bias=neg_max[:], accum_out=total[:])
+        ratio = p_late[:, LATE : LATE + 1]
+        nc.scalar.activation(out=p_early[:], in_=s[:, :EARLY], func=ACT.Exp, bias=neg_early, scale=-1.0, accum_out=early_sum[:])
+        nc.scalar.activation(out=p_late[:], in_=s[:, EARLY:], func=ACT.Exp, bias=neg_max[:], scale=-1.0, accum_out=late_sum[:])
+        nc.vector.tensor_scalar(out=early_rest[:], in0=early_sum[:], scalar1=-1.0, scalar2=None, op0=ALU.add)
+        nc.vector.tensor_scalar(out=total[:], in0=ratio, scalar1=early_rest[:], scalar2=late_sum[:], op0=ALU.mult, op1=ALU.add)
+        nc.vector.tensor_scalar(out=early_gain[:], in0=ratio, scalar1=512.0, scalar2=None, op0=ALU.mult)
         nc.vector.reciprocal(out=inv[:], in_=total[:])
-        for cols in (slice(0, 192), slice(192, J)):
-            nc.vector.tensor_scalar(out=y[:, cols], in0=p[:, cols], scalar1=inv[:], scalar2=512.0, op0=ALU.mult, op1=ALU.mult)
-            nc.sync.dma_start(out=out[:, cols], in_=y[:, cols])
+        nc.vector.tensor_scalar(out=y[:, EARLY:], in0=p_late[:, :LATE], scalar1=inv[:], scalar2=512.0, op0=ALU.mult, op1=ALU.mult)
+        nc.sync.dma_start(out=out[:, EARLY:], in_=y[:, EARLY:])
+        nc.vector.tensor_scalar(out=y[:, :EARLY], in0=p_early[:], scalar1=inv[:], scalar2=early_gain[:], op0=ALU.mult, op1=ALU.mult)
+        nc.sync.dma_start(out=out[:, :EARLY], in_=y[:, :EARLY])

@@ -126,7 +126,7 @@ def tile_attend_spanpointer_kernel(tc, qs, qe, tok_words, tok_scales, offs, offs
         by_vector(b, qe_mx, 768, 896, "bank0")
         by_vector(b, qe_mx, 896, 1024, "bank1")
 
-        OWN, FIRST, EARLY, FILL = 160, 224, 320, 384
+        OWN, FIRST, EARLY, FILL = 160, 224, 288, 384
         LATE = J - EARLY
         s = sb.tile([P, J + 1], F32, name="s")
         neg_early = s[:, J : J + 1]
@@ -170,7 +170,8 @@ def tile_attend_spanpointer_kernel(tc, qs, qe, tok_words, tok_scales, offs, offs
         nc.vector.tensor_scalar(out=total[:], in0=ratio, scalar1=early_rest[:], scalar2=late_sum[:], op0=ALU.mult, op1=ALU.add)
         nc.vector.tensor_scalar(out=early_gain[:], in0=ratio, scalar1=512.0, scalar2=None, op0=ALU.mult)
         nc.vector.reciprocal(out=inv[:], in_=total[:])
+        nc.vector.tensor_scalar(out=y[:, :160], in0=p_early[:, :160], scalar1=inv[:], scalar2=early_gain[:], op0=ALU.mult, op1=ALU.mult)
+        nc.sync.dma_start(out=out[:, :160], in_=y[:, :160])
+        nc.vector.tensor_scalar(out=y[:, 160:EARLY], in0=p_early[:, 160:], scalar1=inv[:], scalar2=early_gain[:], op0=ALU.mult, op1=ALU.mult)
         nc.vector.tensor_scalar(out=y[:, EARLY:], in0=p_late[:, :LATE], scalar1=inv[:], scalar2=512.0, op0=ALU.mult, op1=ALU.mult)
-        nc.sync.dma_start(out=out[:, EARLY:], in_=y[:, EARLY:])
-        nc.vector.tensor_scalar(out=y[:, :EARLY], in0=p_early[:], scalar1=inv[:], scalar2=early_gain[:], op0=ALU.mult, op1=ALU.mult)
-        nc.sync.dma_start(out=out[:, :EARLY], in_=y[:, :EARLY])
+        nc.sync.dma_start(out=out[:, 160:], in_=y[:, 160:])

@@ -158,7 +158,7 @@ def tile_attend_spanpointer_kernel(tc, qs, qe, tok_words, tok_scales, offs, offs
         early_rest = sb.tile([P, 1], F32, name="early_rest")
         late_sum = sb.tile([P, 1], F32, name="late_sum")
         total = sb.tile([P, 1], F32, name="total")
-        early_gain = sb.tile([P, 1], F32, name="early_gain")
+        early_weight = sb.tile([P, EARLY], F32, name="early_weight")
         inv = sb.tile([P, 1], F32, name="inv")
         p_early = sb.tile([P, EARLY], F32, name="p_early")
         p_late = sb.tile([P, LATE + 1], F32, name="p_late")
@@ -168,10 +168,10 @@ def tile_attend_spanpointer_kernel(tc, qs, qe, tok_words, tok_scales, offs, offs
         nc.scalar.activation(out=p_late[:], in_=s[:, EARLY:], func=ACT.Exp, bias=neg_max[:], scale=-1.0, accum_out=late_sum[:])
         nc.vector.tensor_scalar(out=early_rest[:], in0=early_sum[:], scalar1=-1.0, scalar2=None, op0=ALU.add)
         nc.vector.tensor_scalar(out=total[:], in0=ratio, scalar1=early_rest[:], scalar2=late_sum[:], op0=ALU.mult, op1=ALU.add)
-        nc.vector.tensor_scalar(out=early_gain[:], in0=ratio, scalar1=512.0, scalar2=None, op0=ALU.mult)
+        nc.vector.tensor_scalar(out=early_weight[:], in0=p_early[:], scalar1=ratio, scalar2=512.0, op0=ALU.mult, op1=ALU.mult)
         nc.vector.reciprocal(out=inv[:], in_=total[:])
-        nc.vector.tensor_scalar(out=y[:, :160], in0=p_early[:, :160], scalar1=inv[:], scalar2=early_gain[:], op0=ALU.mult, op1=ALU.mult)
+        nc.vector.tensor_scalar(out=y[:, :160], in0=early_weight[:, :160], scalar1=inv[:], scalar2=None, op0=ALU.mult)
         nc.sync.dma_start(out=out[:, :160], in_=y[:, :160])
-        nc.vector.tensor_scalar(out=y[:, 160:EARLY], in0=p_early[:, 160:], scalar1=inv[:], scalar2=early_gain[:], op0=ALU.mult, op1=ALU.mult)
+        nc.scalar.activation(out=y[:, 160:EARLY], in_=early_weight[:, 160:], func=ACT.Copy, scale=inv[:])
         nc.vector.tensor_scalar(out=y[:, EARLY:], in0=p_late[:, :LATE], scalar1=inv[:], scalar2=512.0, op0=ALU.mult, op1=ALU.mult)
         nc.sync.dma_start(out=out[:, 160:], in_=y[:, 160:])

@@ -49,8 +49,11 @@ def tile_attend_spanpointer_kernel(tc, qs, qe, tok_words, tok_scales, offs, offs
         load_scales(nc.sync, 3, 0, T)
         load_scales(nc.sync, 0, T // 2, T)
         nc.sync.dma_start(out=qs_raw[:], in_=qs.rearrange("(p j) q -> p j q", j=PACK))
-        nc.sync.dma_start(out=words[:].bitcast(I32), in_=tok_words[0].bitcast(I32))
-        nc.sync.dma_start(out=qe_raw[:], in_=qe.rearrange("(p j) q -> p j q", j=PACK))
+        nc.sync.dma_start(out=words[:, : T // 2].bitcast(I32), in_=tok_words[0, :, :T].bitcast(I32))
+        nc.sync.dma_start(out=words[:, T // 2 :].bitcast(I32), in_=tok_words[0, :, T:].bitcast(I32))
+        qe_rows = qe.rearrange("(p j) q -> p j q", j=PACK)
+        nc.sync.dma_start(out=qe_raw[:, :2, :], in_=qe_rows[:, :2, :])
+        nc.sync.dma_start(out=qe_raw[:, 2:, :], in_=qe_rows[:, 2:, :])
         nc.sync.dma_start(end_list[:], offs3)
         nc.sync.dma_start(start_list[:], offs2)
 

@@ -98,7 +98,7 @@ def tile_attend_spanpointer_kernel(tc, qs, qe, tok_words, tok_scales, offs, offs
             )
             return bank
 
-        a = sb.tile([P, I], F32, name="a")
+        a = sb.tile([P, I], F32, name="a", tag="a")
         b = sb.tile([P, I], F32, name="b")
 
         qs_bf = cast(qs_raw, "qs_bf")
@@ -126,55 +126,56 @@ def tile_attend_spanpointer_kernel(tc, qs, qe, tok_words, tok_scales, offs, offs
         by_vector(b, qe_mx, 512, 768, "bank5")
         by_scalar(a, qs_mx, 768, 896, "bank6")
         by_scalar(a, qs_mx, 896, 1024, "bank7")
-        by_vector(b, qe_mx, 768, 896, "bank0")
+        by_scalar(b, qe_mx, 768, 896, "bank0")
         by_vector(b, qe_mx, 896, 1024, "bank1")
 
-        OWN, FIRST, EARLY, FILL = 160, 224, 288, 384
-        LATE = J - EARLY
-        s = sb.tile([P, J + 1], F32, name="s")
-        neg_early = s[:, J : J + 1]
-        neg_max = sb.tile([P, 1], F32, name="neg_max")
-        first_starts = sb.tile([P, FIRST - OWN], F32, name="first_starts", tag="first_then_last")
+        OWN, HALF, SUMMED, FIRST_STORE = 192, 256, 384, 160
+        CAP = 64.0
+        s = sb.tile([P, J], F32, name="s")
         starts = sb.tile([P, J], F32, name="starts")
+        last_ends = sb.tile([P, J - SUMMED], F32, name="last_ends")
 
         def offsets(spans, lo, hi):
             return spans[:, lo // LANES : hi // LANES]
 
-        def look_up_and_add(lo, hi, known):
-            nc.vector.tensor_tensor(s[:, lo:hi], b[:].indirect(offsets(end_list, lo, hi)), known, ALU.add)
-
-        nc.scalar.activation(first_starts[:], a[:].indirect(offsets(start_list, OWN, FIRST)), ACT.Copy)
-        for lo, hi in ((FIRST, EARLY), (EARLY, J)):
+        def starts_by_scalar(lo, hi):
             nc.scalar.activation(starts[:, lo:hi], a[:].indirect(offsets(start_list, lo, hi)), ACT.Copy)
-        nc.vector.tensor_copy(starts[:, :OWN], a[:].indirect(offsets(start_list, 0, OWN)))
-        look_up_and_add(OWN, FIRST, first_starts[:])
-        look_up_and_add(0, OWN, starts[:, :OWN])
-        look_up_and_add(FIRST, EARLY, starts[:, FIRST:EARLY])
-        look_up_and_add(EARLY, FILL, starts[:, EARLY:FILL])
-        last_ends = sb.tile([P, J - FILL], F32, name="last_ends", tag="first_then_last")
-        nc.scalar.activation(last_ends[:], b[:].indirect(offsets(end_list, FILL, J)), ACT.Copy)
-        nc.vector.tensor_reduce(out=neg_early, in_=s[:, :EARLY], axis=AX.X, op=ALU.min)
-        nc.vector.tensor_tensor(s[:, FILL:J], last_ends[:], starts[:, FILL:J], ALU.add)
-        nc.vector.tensor_reduce(out=neg_max[:], in_=s[:, EARLY:], axis=AX.X, op=ALU.min)
 
-        early_sum = sb.tile([P, 1], F32, name="early_sum")
-        early_rest = sb.tile([P, 1], F32, name="early_rest")
-        late_sum = sb.tile([P, 1], F32, name="late_sum")
+        def look_up_and_add(lo, hi):
+            nc.vector.tensor_tensor(s[:, lo:hi], b[:].indirect(offsets(end_list, lo, hi)), starts[:, lo:hi], ALU.add)
+
+        starts_by_scalar(OWN, HALF)
+        starts_by_scalar(HALF, SUMMED)
+        nc.scalar.activation(last_ends[:], b[:].indirect(offsets(end_list, SUMMED, J)), ACT.Copy)
+        starts_by_scalar(SUMMED, J)
+        nc.vector.tensor_copy(starts[:, :OWN], a[:].indirect(offsets(start_list, 0, OWN)))
+        look_up_and_add(OWN, HALF)
+        look_up_and_add(0, OWN)
+        look_up_and_add(HALF, SUMMED)
+        nc.vector.tensor_tensor(s[:, SUMMED:], last_ends[:], starts[:, SUMMED:], ALU.add)
+        neg_one = sb.tile([P, 1], F32, name="neg_one", tag="a")
+        neg_two = sb.tile([P, 1], F32, name="neg_two")
+        nc.vector.tensor_reduce(out=neg_one[:], in_=s[:, :HALF], axis=AX.X, op=ALU.min)
+        nc.vector.tensor_reduce(out=neg_two[:], in_=s[:, HALF:], axis=AX.X, op=ALU.min)
+
+        lead = sb.tile([P, 1], F32, name="lead")
+        ratio = sb.tile([P, 1], F32, name="ratio")
+        sum_one = sb.tile([P, 1], F32, name="sum_one")
+        sum_two = sb.tile([P, 1], F32, name="sum_two")
         total = sb.tile([P, 1], F32, name="total")
-        early_weight = sb.tile([P, EARLY], F32, name="early_weight")
         inv = sb.tile([P, 1], F32, name="inv")
-        p_early = sb.tile([P, EARLY], F32, name="p_early")
-        p_late = sb.tile([P, LATE + 1], F32, name="p_late")
+        p = sb.tile([P, J], F32, name="p")
+        weight_one = sb.tile([P, HALF], F32, name="weight_one")
         y = sb.tile([P, J], F32, name="y")
-        ratio = p_late[:, LATE : LATE + 1]
-        nc.scalar.activation(out=p_early[:], in_=s[:, :EARLY], func=ACT.Exp, bias=neg_early, scale=-1.0, accum_out=early_sum[:])
-        nc.scalar.activation(out=p_late[:], in_=s[:, EARLY:], func=ACT.Exp, bias=neg_max[:], scale=-1.0, accum_out=late_sum[:])
-        nc.vector.tensor_scalar(out=early_rest[:], in0=early_sum[:], scalar1=-1.0, scalar2=None, op0=ALU.add)
-        nc.vector.tensor_scalar(out=total[:], in0=ratio, scalar1=early_rest[:], scalar2=late_sum[:], op0=ALU.mult, op1=ALU.add)
-        nc.vector.tensor_scalar(out=early_weight[:], in0=p_early[:], scalar1=ratio, scalar2=512.0, op0=ALU.mult, op1=ALU.mult)
+        nc.scalar.activation(out=p[:, :HALF], in_=s[:, :HALF], func=ACT.Exp, bias=neg_one[:], scale=-1.0, accum_out=sum_one[:])
+        nc.scalar.activation(out=p[:, HALF:], in_=s[:, HALF:], func=ACT.Exp, bias=neg_two[:], scale=-1.0, accum_out=sum_two[:])
+        nc.vector.tensor_scalar(out=lead[:], in0=neg_two[:], scalar1=neg_one[:], scalar2=CAP, op0=ALU.subtract, op1=ALU.min)
+        nc.scalar.activation(out=ratio[:], in_=lead[:], func=ACT.Exp)
+        nc.vector.tensor_scalar(out=total[:], in0=ratio[:], scalar1=sum_one[:], scalar2=sum_two[:], op0=ALU.mult, op1=ALU.add)
+        nc.vector.tensor_scalar(out=weight_one[:], in0=p[:, :HALF], scalar1=ratio[:], scalar2=512.0, op0=ALU.mult, op1=ALU.mult)
         nc.vector.reciprocal(out=inv[:], in_=total[:])
-        nc.vector.tensor_scalar(out=y[:, :160], in0=early_weight[:, :160], scalar1=inv[:], scalar2=None, op0=ALU.mult)
-        nc.sync.dma_start(out=out[:, :160], in_=y[:, :160])
-        nc.scalar.activation(out=y[:, 160:EARLY], in_=early_weight[:, 160:], func=ACT.Copy, scale=inv[:])
-        nc.vector.tensor_scalar(out=y[:, EARLY:], in0=p_late[:, :LATE], scalar1=inv[:], scalar2=512.0, op0=ALU.mult, op1=ALU.mult)
-        nc.sync.dma_start(out=out[:, 160:], in_=y[:, 160:])
+        nc.vector.tensor_scalar(out=y[:, :FIRST_STORE], in0=weight_one[:, :FIRST_STORE], scalar1=inv[:], scalar2=None, op0=ALU.mult)
+        nc.sync.dma_start(out=out[:, :FIRST_STORE], in_=y[:, :FIRST_STORE])
+        nc.scalar.activation(out=y[:, FIRST_STORE:HALF], in_=weight_one[:, FIRST_STORE:], func=ACT.Copy, scale=inv[:])
+        nc.vector.tensor_scalar(out=y[:, HALF:], in0=p[:, HALF:], scalar1=inv[:], scalar2=512.0, op0=ALU.mult, op1=ALU.mult)
+        nc.sync.dma_start(out=out[:, FIRST_STORE:], in_=y[:, FIRST_STORE:])

@@ -98,7 +98,7 @@ def tile_attend_spanpointer_kernel(tc, qs, qe, tok_words, tok_scales, offs, offs
             )
             return bank
 
-        a = sb.tile([P, I], F32, name="a", tag="a")
+        a = sb.tile([P, I], F32, name="a")
         b = sb.tile([P, I], F32, name="b")
 
         qs_bf = cast(qs_raw, "qs_bf")
@@ -130,7 +130,7 @@ def tile_attend_spanpointer_kernel(tc, qs, qe, tok_words, tok_scales, offs, offs
         by_vector(b, qe_mx, 896, 1024, "bank1")
 
         OWN, HALF, SUMMED, FIRST_STORE = 192, 256, 384, 160
-        CAP = 64.0
+        CAP = 2.0**90
         s = sb.tile([P, J], F32, name="s")
         starts = sb.tile([P, J], F32, name="starts")
         last_ends = sb.tile([P, J - SUMMED], F32, name="last_ends")
@@ -153,13 +153,14 @@ def tile_attend_spanpointer_kernel(tc, qs, qe, tok_words, tok_scales, offs, offs
         look_up_and_add(0, OWN)
         look_up_and_add(HALF, SUMMED)
         nc.vector.tensor_tensor(s[:, SUMMED:], last_ends[:], starts[:, SUMMED:], ALU.add)
-        neg_one = sb.tile([P, 1], F32, name="neg_one", tag="a")
+        neg_one = a[:, 0:1]
         neg_two = sb.tile([P, 1], F32, name="neg_two")
-        nc.vector.tensor_reduce(out=neg_one[:], in_=s[:, :HALF], axis=AX.X, op=ALU.min)
+        nc.vector.tensor_reduce(out=neg_one, in_=s[:, :HALF], axis=AX.X, op=ALU.min)
         nc.vector.tensor_reduce(out=neg_two[:], in_=s[:, HALF:], axis=AX.X, op=ALU.min)
 
-        lead = sb.tile([P, 1], F32, name="lead")
         ratio = sb.tile([P, 1], F32, name="ratio")
+        factor_one = sb.tile([P, 1], F32, name="factor_one")
+        share_one = sb.tile([P, 1], F32, name="share_one")
         sum_one = sb.tile([P, 1], F32, name="sum_one")
         sum_two = sb.tile([P, 1], F32, name="sum_two")
         total = sb.tile([P, 1], F32, name="total")
@@ -167,12 +168,13 @@ def tile_attend_spanpointer_kernel(tc, qs, qe, tok_words, tok_scales, offs, offs
         p = sb.tile([P, J], F32, name="p")
         weight_one = sb.tile([P, HALF], F32, name="weight_one")
         y = sb.tile([P, J], F32, name="y")
-        nc.scalar.activation(out=p[:, :HALF], in_=s[:, :HALF], func=ACT.Exp, bias=neg_one[:], scale=-1.0, accum_out=sum_one[:])
+        nc.scalar.activation(out=p[:, :HALF], in_=s[:, :HALF], func=ACT.Exp, bias=neg_one, scale=-1.0, accum_out=sum_one[:])
+        nc.scalar.activation(out=ratio[:], in_=neg_one, func=ACT.Exp, bias=neg_two[:], scale=-1.0)
         nc.scalar.activation(out=p[:, HALF:], in_=s[:, HALF:], func=ACT.Exp, bias=neg_two[:], scale=-1.0, accum_out=sum_two[:])
-        nc.vector.tensor_scalar(out=lead[:], in0=neg_two[:], scalar1=neg_one[:], scalar2=CAP, op0=ALU.subtract, op1=ALU.min)
-        nc.scalar.activation(out=ratio[:], in_=lead[:], func=ACT.Exp)
-        nc.vector.tensor_scalar(out=total[:], in0=ratio[:], scalar1=sum_one[:], scalar2=sum_two[:], op0=ALU.mult, op1=ALU.add)
-        nc.vector.tensor_scalar(out=weight_one[:], in0=p[:, :HALF], scalar1=ratio[:], scalar2=512.0, op0=ALU.mult, op1=ALU.mult)
+        nc.vector.tensor_scalar(out=share_one[:], in0=ratio[:], scalar1=CAP, scalar2=sum_one[:], op0=ALU.min, op1=ALU.mult)
+        nc.vector.tensor_scalar(out=factor_one[:], in0=ratio[:], scalar1=CAP, scalar2=512.0, op0=ALU.min, op1=ALU.mult)
+        nc.vector.tensor_tensor(total[:], share_one[:], sum_two[:], ALU.add)
+        nc.vector.tensor_scalar(out=weight_one[:], in0=p[:, :HALF], scalar1=factor_one[:], scalar2=None, op0=ALU.mult)
         nc.vector.reciprocal(out=inv[:], in_=total[:])
         nc.vector.tensor_scalar(out=y[:, :FIRST_STORE], in0=weight_one[:, :FIRST_STORE], scalar1=inv[:], scalar2=None, op0=ALU.mult)
         nc.sync.dma_start(out=out[:, :FIRST_STORE], in_=y[:, :FIRST_STORE])

from contextlib import ExitStack

import concourse.mybir as mybir

D, T, I, J, Q = 512, 2048, 1024, 512, 128
FLOPS = 2 * 2 * D * Q * I

F32 = mybir.dt.float32
BF16 = mybir.dt.bfloat16
I32 = mybir.dt.int32
U32 = mybir.dt.uint32
U16 = mybir.dt.uint16
U8 = mybir.dt.uint8
FP8X4 = mybir.dt.float8_e4m3fn_x4
FP4X4 = mybir.dt.float4_e2m1fn_x4
ACT = mybir.ActivationFunctionType
ALU = mybir.AluOpType
AX = mybir.AxisListType

P = 128
PACK = 4
LANES = 16
QUARTER = I // 4


def tile_attend_spanpointer_kernel(tc, qs, qe, tok_words, tok_scales, offs, offs2, offs3, out):
    nc = tc.nc
    with ExitStack() as ctx:
        sb = ctx.enter_context(tc.tile_pool(name="sb", bufs=1))
        ps = ctx.enter_context(tc.psum_pool(name="ps", bufs=1))

        words = sb.tile([P, T], U16, name="words", align_bytes=64)
        scales = sb.tile([P, T], U8, name="scales", align_bytes=64)
        tok_list = sb.tile([P, I // LANES], U16, name="tok_list")
        start_list = sb.tile([P, J // LANES], U16, name="start_list")
        end_list = sb.tile([P, J // LANES], U16, name="end_list")
        qs_raw = sb.tile([P, PACK, Q], F32, name="qs_raw", tag="qs_raw", align_bytes=64)
        qe_raw = sb.tile([P, PACK, Q], F32, name="qe_raw", tag="qe_raw", align_bytes=64)

        def load_scales(queue, g, lo, hi):
            queue.dma_start(out=scales[g:P:32, lo:hi].bitcast(I32), in_=tok_scales[0, g:16:4, lo:hi].bitcast(I32))

        nc.vector.memset(scales[:, : T // 2].bitcast(I32), 0)
        nc.vector.memset(scales[:, T // 2 :].bitcast(I32), 0)
        nc.sync.dma_start(tok_list[:], offs)
        load_scales(nc.sync, 0, 0, T // 2)
        load_scales(nc.scalar, 1, 0, T)
        load_scales(nc.sync, 2, 0, T)
        load_scales(nc.sync, 3, 0, T)
        load_scales(nc.sync, 0, T // 2, T)
        nc.sync.dma_start(out=qs_raw[:], in_=qs.rearrange("(p j) q -> p j q", j=PACK))
        nc.sync.dma_start(out=words[:, : T // 2].bitcast(I32), in_=tok_words[0, :, :T].bitcast(I32))
        nc.sync.dma_start(out=words[:, T // 2 :].bitcast(I32), in_=tok_words[0, :, T:].bitcast(I32))
        qe_rows = qe.rearrange("(p j) q -> p j q", j=PACK)
        nc.sync.dma_start(out=qe_raw[:, :2, :], in_=qe_rows[:, :2, :])
        nc.sync.dma_start(out=qe_raw[:, 2:, :], in_=qe_rows[:, 2:, :])
        nc.sync.dma_start(end_list[:], offs3)
        nc.sync.dma_start(start_list[:], offs2)

        def cast(raw, name):
            grouped = sb.tile([P, Q, PACK], BF16, name=name, tag=name, align_bytes=64)
            nc.scalar.copy(
                out=grouped[:].rearrange("p (c i) j -> p c j i", i=4),
                in_=raw[:].rearrange("p j (c i) -> p c j i", i=4),
            )
            return grouped

        def quantise(grouped, name):
            codes = sb.tile([P, Q], U32, name=name + "_codes", align_bytes=64)
            plane = sb.tile([P, Q], U8, name=name + "_scales", align_bytes=64)
            nc.vector.quantize_mx(out=codes[:].bitcast(FP8X4), scales=plane[:], in_=grouped[:].rearrange("p q j -> p (q j)"))
            return codes, plane

        def gather(dst, window, lo, hi):
            nc.vector.tensor_copy(dst, window[:].indirect(tok_list[:, lo // LANES : hi // LANES]))

        picked_words = []

        def gather_words(tag, quarters):
            piece = sb.tile([P, quarters, QUARTER], U16, name="picked_" + tag, tag=tag, align_bytes=64)
            for k in range(quarters):
                c = len(picked_words)
                gather(piece[:, k, :], words, c * QUARTER, (c + 1) * QUARTER)
                picked_words.append(piece[:, k, :])

        def score(query, lo, hi, bank_name):
            codes, plane = query
            bank = ps.tile([P, hi - lo], F32, name=bank_name)
            c = lo // QUARTER
            nc.tensor.matmul_mx(
                out=bank[:],
                lhsT=codes[:].bitcast(FP8X4),
                lhsT_scale=plane[:],
                rhs=picked_words[c][:, lo - c * QUARTER : hi - c * QUARTER].bitcast(FP4X4),
                rhs_scale=picked_scales[:, lo:hi],
                start=True,
                stop=True,
            )
            return bank

        a = sb.tile([P, I], F32, name="a")
        b = sb.tile([P, I], F32, name="b")

        qs_bf = cast(qs_raw, "qs_bf")
        qe_bf = cast(qe_raw, "qe_bf")

        picked_scales = sb.tile([P, I], U8, name="picked_scales", align_bytes=64)
        gather(picked_scales[:], scales, 0, I)
        gather_words("words_first", 1)
        qs_mx = quantise(qs_bf, "qs")
        gather_words("qs_raw", 1)
        qe_mx = quantise(qe_bf, "qe")
        gather_words("qe_raw", 2)

        def by_scalar(dst, query, lo, hi, bank_name):
            nc.scalar.activation(out=dst[:, lo:hi], in_=score(query, lo, hi, bank_name)[:], func=ACT.Copy, scale=-1.0)

        def by_vector(dst, query, lo, hi, bank_name):
            nc.vector.tensor_scalar(out=dst[:, lo:hi], in0=score(query, lo, hi, bank_name)[:], scalar1=-1.0, scalar2=None, op0=ALU.mult)

        by_scalar(a, qs_mx, 0, 256, "bank0")
        by_scalar(a, qs_mx, 256, 512, "bank1")
        by_scalar(b, qe_mx, 0, 256, "bank2")
        by_scalar(b, qe_mx, 256, 512, "bank3")
        by_scalar(a, qs_mx, 512, 768, "bank4")
        by_vector(b, qe_mx, 512, 768, "bank5")
        by_scalar(a, qs_mx, 768, 896, "bank6")
        by_scalar(a, qs_mx, 896, 1024, "bank7")
        by_scalar(b, qe_mx, 768, 896, "bank0")
        by_vector(b, qe_mx, 896, 1024, "bank1")

        OWN, HALF, SUMMED, FIRST_STORE = 192, 256, 384, 160
        CAP = 2.0**90
        s = sb.tile([P, J], F32, name="s")
        starts = sb.tile([P, J], F32, name="starts")
        last_ends = sb.tile([P, J - SUMMED], F32, name="last_ends")

        def offsets(spans, lo, hi):
            return spans[:, lo // LANES : hi // LANES]

        def starts_by_scalar(lo, hi):
            nc.scalar.activation(starts[:, lo:hi], a[:].indirect(offsets(start_list, lo, hi)), ACT.Copy)

        def look_up_and_add(lo, hi):
            nc.vector.tensor_tensor(s[:, lo:hi], b[:].indirect(offsets(end_list, lo, hi)), starts[:, lo:hi], ALU.add)

        starts_by_scalar(OWN, HALF)
        starts_by_scalar(HALF, SUMMED)
        nc.scalar.activation(last_ends[:], b[:].indirect(offsets(end_list, SUMMED, J)), ACT.Copy)
        starts_by_scalar(SUMMED, J)
        nc.vector.tensor_copy(starts[:, :OWN], a[:].indirect(offsets(start_list, 0, OWN)))
        look_up_and_add(OWN, HALF)
        look_up_and_add(0, OWN)
        look_up_and_add(HALF, SUMMED)
        nc.vector.tensor_tensor(s[:, SUMMED:], last_ends[:], starts[:, SUMMED:], ALU.add)
        neg_one = a[:, 0:1]
        neg_two = sb.tile([P, 1], F32, name="neg_two")
        nc.vector.tensor_reduce(out=neg_one, in_=s[:, :HALF], axis=AX.X, op=ALU.min)
        nc.vector.tensor_reduce(out=neg_two[:], in_=s[:, HALF:], axis=AX.X, op=ALU.min)

        ratio = sb.tile([P, 1], F32, name="ratio")
        factor_one = sb.tile([P, 1], F32, name="factor_one")
        share_one = sb.tile([P, 1], F32, name="share_one")
        sum_one = sb.tile([P, 1], F32, name="sum_one")
        sum_two = sb.tile([P, 1], F32, name="sum_two")
        total = sb.tile([P, 1], F32, name="total")
        inv = sb.tile([P, 1], F32, name="inv")
        p = sb.tile([P, J], F32, name="p")
        weight_one = sb.tile([P, HALF], F32, name="weight_one")
        y = sb.tile([P, J], F32, name="y")
        nc.scalar.activation(out=p[:, :HALF], in_=s[:, :HALF], func=ACT.Exp, bias=neg_one, scale=-1.0, accum_out=sum_one[:])
        nc.scalar.activation(out=ratio[:], in_=neg_one, func=ACT.Exp, bias=neg_two[:], scale=-1.0)
        nc.scalar.activation(out=p[:, HALF:], in_=s[:, HALF:], func=ACT.Exp, bias=neg_two[:], scale=-1.0, accum_out=sum_two[:])
        nc.vector.tensor_scalar(out=share_one[:], in0=ratio[:], scalar1=CAP, scalar2=sum_one[:], op0=ALU.min, op1=ALU.mult)
        nc.vector.tensor_scalar(out=factor_one[:], in0=ratio[:], scalar1=CAP, scalar2=512.0, op0=ALU.min, op1=ALU.mult)
        nc.vector.tensor_tensor(total[:], share_one[:], sum_two[:], ALU.add)
        nc.vector.tensor_scalar(out=weight_one[:], in0=p[:, :HALF], scalar1=factor_one[:], scalar2=None, op0=ALU.mult)
        nc.vector.reciprocal(out=inv[:], in_=total[:])
        nc.vector.tensor_scalar(out=y[:, :FIRST_STORE], in0=weight_one[:, :FIRST_STORE], scalar1=inv[:], scalar2=None, op0=ALU.mult)
        nc.sync.dma_start(out=out[:, :FIRST_STORE], in_=y[:, :FIRST_STORE])
        nc.scalar.activation(out=y[:, FIRST_STORE:HALF], in_=weight_one[:, FIRST_STORE:], func=ACT.Copy, scale=inv[:])
        nc.vector.tensor_scalar(out=y[:, HALF:], in0=p[:, HALF:], scalar1=inv[:], scalar2=512.0, op0=ALU.mult, op1=ALU.mult)
        nc.sync.dma_start(out=out[:, FIRST_STORE:], in_=y[:, FIRST_STORE:])
